import numpy as np, ml_dtypes
CORES = [2,3,42,43,82,83,122,123]
N = 8
R, T, B, CAPP = 8192, 4096, 128, 1024
LOW = np.float32(-201 * 2.0 ** 92)
def entries(a): return a.T.reshape(-1)
def pack(v, P): return np.ascontiguousarray(np.asarray(v, np.int32).reshape(-1, P).T)
def table(rng, how, c=()):
    t = rng.standard_normal((N, 128, R), dtype=np.float32); k = np.arange(128) if how == "neg" else rng.permutation(128)[:16]
    t[:, k] = -0.125 - np.abs(t[:, k])
    if len(c): t[(c // R)[:, None], rng.permutation(128)[:16][None, :], (c % R)[:, None]] = LOW
    return t.astype(ml_dtypes.bfloat16)
def lists(rng, how):
    O = np.stack([rng.permutation(np.repeat(np.arange(N), CAPP))[:T] for r in range(N)])
    if how in ("astride", "early"): P = rng.permutation(N)[:T // CAPP]; O = np.stack([rng.permutation(np.repeat(P, CAPP)) for r in range(N)])
    I = R * O + rng.integers(0, R, (N, T))
    if how == "late": u = rng.random((N, T)); I = np.where(u < 0.5, R * O + np.where(u < 0.25, 0, R - 1), I)
    s = np.concatenate([[0], rng.integers(1 - T // 2, T // 2 + 1, N - 1), [int(rng.integers(1 - T // 2, 1))]])
    if how == "astride":
        z = int(rng.integers(1, N - 1)); k = int(rng.integers(0, B - 1)); s[1:z] = -rng.integers(1, T, z - 1); s[z] = -T; s[z + 1] = T; s[z + 2:N] = rng.integers(1, T, N - z - 2); s[N] = 0
    if how == "early": s[1:] = -T
    if how == "late": s[1:N] = T; s[N] = 0
    if how == "void":
        w = int(rng.integers(3, N - 1)); z = int(rng.integers(1, w - 1)); s[z] = int(rng.integers(1, T // 2 + 1)); s[z + 1] = s[z] - T; s[w:] = s[w] - T * np.arange(N + 1 - w)
    S = T * np.arange(N + 1) + s
    E = np.concatenate([np.append(np.sort(rng.integers(S[q], S[q + 1] + 1, B - 1)), S[q + 1]) for q in range(N)])
    if how == "astride":
        E[B * z:B * z + B - 1] = np.concatenate([np.sort(rng.integers(S[z], T * z - T // 2 + 1, k)), np.sort(rng.integers(T * z + T + T // 2, S[z + 1], B - 2 - k)), [S[z + 1] - 1]])
        L = max(N * T - 1, S[N - 1]); E[N * B - B:N * B - 1] = np.minimum(E[N * B - B:N * B - 1], L); E[N * B - 2] = L
        E += np.isin(E, np.setdiff1d(T * np.arange(1, N), S[z:z + 2]))
    if how == "neg":
        K = rng.random(N * B) < 0.5; K[0] = False; K[B - 1::B] = True; j = np.flatnonzero(K); E = E[j[np.searchsorted(j, np.arange(N * B))]]
    if how == "void":
        k = np.sort(np.stack([B * q + 1 + rng.permutation(B - 2)[:3] for q in range(N)]), axis=1); v = E[k]; v[:, 2] = S[1:]
        E = np.concatenate([[0], v.reshape(-1)])[np.searchsorted(k.reshape(-1), np.arange(N * B), side="right")]
    d = {"idx": np.stack([pack(i, 16) for i in I]), "end": np.stack([pack(E, 16)] * N)}
    if how == "neg":
        n = np.diff(np.concatenate([[0], E])).reshape(N, B); b = B * np.arange(N) + ((n > 0) * (1 + rng.random((N, B)))).argmax(axis=1)
        d["tab"] = table(rng, "neg", I.reshape(-1)[np.isin(np.searchsorted(E, np.arange(N * T), side="right"), b)])
    return d
def setup_inputs(rng):
    return dict({"tab": table(rng, "uniform")}, **lists(rng, "uniform"))
def setup_inputs_astride(rng):
    d = setup_inputs(rng); d.update(lists(rng, "astride"))
    for k in ("tab",): d[k] = (d[k].astype(np.float32) * 1048576.0).astype(d[k].dtype)
    return d
def setup_inputs_early(rng):
    d = setup_inputs(rng); d.update(lists(rng, "early"))
    for k in ("tab",): d[k] = (d[k].astype(np.float32) * (1 / 1024.0)).astype(d[k].dtype)
    return d
def setup_inputs_late(rng):
    d = setup_inputs(rng); d.update(lists(rng, "late"))
    return d
def setup_inputs_neg(rng):
    d = setup_inputs(rng); d.update(lists(rng, "neg"))
    return d
def setup_inputs_void(rng):
    d = setup_inputs(rng); d.update(lists(rng, "void"))
    return d
def check_inputs(x):
    bad = []
    if x["idx"].min() < 0 or x["idx"].max() >= N * R: bad.append("idx out of range")
    if x["end"].min() < 0 or x["end"].max() >= N * T + 1: bad.append("end out of range")
    if (x["end"] != x["end"][:1]).any(): bad.append("end differs from rank to rank")
    v = entries(x["end"][0]).astype(np.int64); s = v[B - 1::B]
    if (np.diff(v) < 0).any(): bad.append("end falls")
    if any(s[q - 1] > T * (q + 1) or (s[q - 1] < T * (q - 1) and s[q - 1] != s[N - 1]) for q in range(1, N)): bad.append("an entry belongs to a bag of a rank that is more than one away from its holder")
    if max(int(np.bincount(entries(a) // R, minlength=N).max()) for a in x["idx"]) > CAPP: bad.append("more than CAPP entries of a rank's idx point into one rank's part of the table")
    t = x["tab"].astype(np.float32)
    if t.min() < np.float32(-1e30) or t.max() > np.float32(1e30): bad.append("tab beyond -1e30 to 1e30")
    return bad
def reference(tab, idx, end):
    A = np.concatenate(list(tab), axis=1)
    G = A[:, np.concatenate([entries(a) for a in idx])]
    Y = np.zeros((128, N * B), tab.dtype)
    for r in range(N):
        c = np.concatenate([[0], entries(end[r])])
        for b in range(B * r, B * r + B):
            if c[b + 1] > c[b]: Y[:, b] = G[:, c[b]:c[b + 1]].max(axis=1)
    return {"y": np.stack([Y[:, B * r:B * r + B] for r in range(N)])}

@@ -1,0 +1,405 @@
+from concourse.bass import DstId, RemoteDMATransfer
+from concourse.mybir import AluOpType as ALU, ActivationFunctionType as ACT
+NR = 8
+HS = 4
+LOW = -201.0 * 2.0 ** 92
+NCORES = 128
+KC = ["i16", "cdv", "iota_a", "dwr", "dlt", "e0", "e1", "em", "tri", "rep", "cb1", "cb2", "cd1", "cd2", "k1", "selx", "zt", "zz"]
+KF = ["basew", "trash", "pm", "ne", "xx", "x2"]
+SPEC = {
+    "float32": "cst 8,kf 6 64,pc 272,zsb 144,pay 4 32,msg 8 12,land 10 12,qm 4 8,lf 128",
+    "bfloat16": "kc 18 128,tabx 8208,iota_b 64,zo 2 256,zs 136,osel 8,selw 8 128,selp 8 128,gge 256,sx 272,msk 2 384,col 3 32,"
+                "oa 32 128,ob1 32 64,ob2 32 64,lhl 2 64,qhl 2 8,flg 9344,lowt 1024,gt 8192,sc 8208,part 8 128,pland 16 128,ysb 128",
+    "int32": "idxa 256,idxe 32,pidx 4,pv 32,ti 32", "float16": "gd 256,mg 384", "uint16": "cof 32,offs 512,lfu 128"}
+SCRATCH = {}
+for _dt in SPEC:
+    for _e in SPEC[_dt].split(","):
+        _w = _e.split()
+        SCRATCH[_w[0]] = ("sbuf", [128] + [int(x) for x in _w[1:]], _dt)
+for _n, _sh, _dt in (("endw", [16, 64], "int32"), ("onef", [16, 128], "float32"), ("id16", [16, 16], "float32"),
+                     ("ei", [16, 4, 32], "int32"), ("cbf", [16, 24], "bfloat16"), ("rbf", [16, 24], "bfloat16"),
+                     ("rdg", [16, 24, 16], "bfloat16"), ("ef", [16, 9], "float32"), ("zdg", [16, 9, 16], "float32")):
+    SCRATCH[_n] = ("sbuf", _sh, _dt)
+for _n in ("pd", "pp", "pa", "pr", "px", "pn", "po", "pq"):
+    SCRATCH[_n] = ("psum", [128, 512], "float32")
+SEMAPHORES = ["v", "s", "p", "gi", "ia", "ie", "en", "tb0", "tb1", "tb2", "tb3", "yd", "arl", "loc", "taba"] + ["pa%d" % i for i in range(16)]
+
+
+def bits(m):
+    return [i for i in range(16) if (m >> i) & 1]
+
+
+def emask(es):
+    return sum(1 << e for e in es)
+
+
+def plan(T, topo):
+    cores = list(T.cores)
+    parts = [(cores[o], o, 0, HS) for o in range(NR)]
+    used = []
+    if HS < NR:
+        for o in range(NR):
+            h = [c for c in range(NCORES) if topo.chip(c) == topo.chip(cores[o]) and c not in cores and c not in used
+                 and all(topo.may_write(c, d) for d in cores)][0]
+            used.append(h)
+            parts.append((h, o, HS, NR))
+    return [p + ([q for q in range(NR) if q + 1 >= p[2] and q - 1 < p[3]],) for p in parts]
+
+
+def ready(part, q):
+    return min(q + 1, part[3] - 1) - part[2]
+
+
+def groups(part):
+    ns = part[3] - part[2]
+    a = [q for q in part[4] if ready(part, q) < ns - 1]
+    b = [q for q in part[4] if ready(part, q) == ns - 1]
+    return [x for x in (a, b) if x]
+
+
+def engines(topo, cores, part, grp):
+    dst = [q for q in grp if cores[q] != part[0]]
+    if not dst:
+        return {}
+    pool = bits(topo.mask(part[0], cores[dst[0]]))
+    for q in dst:
+        pool = [e for e in pool if e in bits(topo.mask(part[0], cores[q]))]
+    n = 1
+    while 2 * n * len(dst) <= min(len(pool), 8):
+        n *= 2
+    return {q: pool[n * i:n * i + n] for i, q in enumerate(dst)}
+
+
+def table_engines(topo, a, b):
+    hm = bits(topo.mask(a, b))
+    return hm[len(hm) // 2:]
+
+
+def rank_program(g, core, T, topo):
+    cores = list(T.cores)
+    parts = plan(T, topo)
+    rank = T.rank_of(core)
+    mine = [p for p in parts if p[0] == core]
+    if not mine:
+        return
+    part = mine[0]
+    own, s0, s1, blocks = part[1], part[2], part[3], part[4]
+    ns, nq, qlo = s1 - s0, len(blocks), blocks[0]
+    n8 = 8 * nq
+    Q = {"v": g.vector, "s": g.scalar, "p": g.tensor, "g": g, "y": g.sync}
+    SEM = {"v": "v", "s": "s", "p": "p", "g": "gi"}
+    cnt = {"v": 0, "s": 0, "p": 0, "gi": 0, "loc": 0}
+    seen = {}
+
+    def need(q, *toks):
+        best = {}
+        for t in toks:
+            if t is not None:
+                best[t[0]] = max(best.get(t[0], 0), t[1])
+        for sem in best:
+            if seen.get((q, sem), 0) < best[sem]:
+                Q[q].wait_ge(T.sem[sem], best[sem])
+                seen[(q, sem)] = best[sem]
+
+    def do(q, call, *args, **kw):
+        sem = SEM[q]
+        call(*args, **kw).then_inc(T.sem[sem], 1)
+        cnt[sem] += 1
+        return (sem, cnt[sem])
+
+    V, S, P = g.vector, g.scalar, g.tensor
+
+    def vts(out, in0, a, b, op0, op1=None, w=()):
+        need("v", *w)
+        if op1 is None:
+            return do("v", V.tensor_scalar, out, in0, a, b, op0)
+        return do("v", V.tensor_scalar, out, in0, a, b, op0, op1)
+
+    def vtt(out, a, b, op, w=()):
+        need("v", *w)
+        return do("v", V.tensor_tensor, out, a, b, op)
+
+    def vcp(out, a, w=()):
+        need("v", *w)
+        return do("v", V.tensor_copy, out, a)
+
+    def vms(ap, c, w=()):
+        need("v", *w)
+        return do("v", V.memset, ap, c)
+
+    def act(out, in_, func, w=(), **kw):
+        need("s", *w)
+        return do("s", S.activation, out, in_, func, **kw)
+
+    def mm(out, l, r, start, stop, w=()):
+        need("p", *w)
+        return do("p", P.matmul, out, l, r, start, stop)
+
+    def iota(out, pat, base, cm, flag=True):
+        if flag:
+            return do("g", g.iota, out, pat, base, cm, allow_small_or_imprecise_dtypes=True)
+        return do("g", g.iota, out, pat, base, cm)
+
+    def dst(c):
+        a = topo.addr(c)
+        return DstId(rid=a[0], pnc=a[1])
+
+    def C(n, p=128, a=0, b=128):
+        return T.kc[0:p, KC.index(n), a:b]
+
+    def F(n):
+        return T.kf[:, KF.index(n), 0:n8]
+
+    helper = [p[0] for p in parts if p[1] == own and p[0] != core and rank is not None]
+    IA, IE, EN = ("ia", 128), ("ie", 16), ("en", 16)
+    if rank is not None:
+        for o in range(4):
+            g.sync.dma_start(T.idxa[16 * o:16 * o + 16, :], T.idx[:]).then_inc(T.sem.ia, 16)
+            g.scalar.dma_start(T.idxa[64 + 16 * o:80 + 16 * o, :], T.idx[:]).then_inc(T.sem.ia, 16)
+        g.scalar.dma_start(T.endw[:], T.end[:]).then_inc(T.sem.en, 16)
+        g.sync.dma_start(T.idxe[:], T.idx[:]).then_inc(T.sem.ie, 16)
+        for k in range(4):
+            g.sync.dma_start(T.tabx[:, 2048 * k:2048 * k + 2048], T.tab[:, 2048 * k:2048 * k + 2048]).then_inc(T.sem["tb%d" % k], 16)
+    pidx, cst = T.pidx, T.cst
+    if rank is not None:
+        g_pi = iota(pidx[:, 0:1], [[0, 1]], 0, 1, False)
+        g_16 = iota(C("i16"), [[0, 8], [1, 16]], 0, 0)
+        g_cd = iota(C("cdv"), [[-1, 8], [0, 16]], 0, 0)
+        g_ia = iota(C("iota_a"), [[1, 128]], 0, 0)
+        g_ib = iota(T.iota_b[:], [[-128, 64]], 0, 0)
+    g_dw = iota(C("dwr"), [[0, 8], [-1, 16]], 0, 1)
+    g_bm = iota(T.qm[:, 3, 0:nq], [[1024, nq]], 1024 * (qlo - 1 - s0), 0)
+    g_bw = iota(F("basew"), [[1024, nq], [0, 8]], 1024 * (qlo - 1 - s0), 0)
+    g_tr = iota(F("trash"), [[16, n8]], 16 + 1024 * ns, 1)
+    t_ef = t_id = None
+    local, t_ld = False, None
+    if rank is not None:
+        if helper:
+            hm = table_engines(topo, core, helper[0])
+            for k in range(4):
+                need("g", ("tb%d" % k, 16))
+                a = topo.addr(helper[0])
+                g.remote_dma(T.tabx[:, 2048 * k:2048 * k + 2048], T.tabx[:, 2048 * k:2048 * k + 2048], T.sem.taba, T.sem.loc,
+                             a[1], a[0], emask(hm))
+                cnt["loc"] += len(hm)
+        oi = vts(pidx[:, 1:2], pidx[:, 0:1], 4, None, ALU.arith_shift_right, w=[g_pi])
+        ri = vts(pidx[:, 2:3], pidx[:, 0:1], 15, None, ALU.bitwise_and)
+        vms(T.zo[:, 0, :], 0.0)
+        vms(T.zo[:, 1, :], 1.0)
+        c_sx0 = vms(T.sx[:, 0:1], 0.0)
+        c_of = vcp(cst[:, 0:1], pidx[:, 1:2], w=[oi])
+        c_th = vts(cst[:, 2:3], pidx[:, 1:2], 8192.0, None, ALU.mult)
+        c_rf = vcp(cst[:, 1:2], pidx[:, 2:3], w=[ri])
+        c_nr = vts(cst[:, 3:4], pidx[:, 2:3], -1.0, None, ALU.mult)
+        c_zs = vms(T.zs[:], 0.0)
+        vms(C("k1", 1, 0, 16), 0.0)
+        c_k1 = vms(C("k1", 1, 16, 128), 1024.0)
+        d_ = vts(C("dlt"), C("cdv"), cst[:, 0:1], None, ALU.add, w=[g_cd, c_of])
+        vts(C("tri"), C("i16"), cst[:, 1:2], None, ALU.is_gt, w=[g_16, c_rf])
+        rep = vts(C("rep"), C("i16"), cst[:, 1:2], None, ALU.is_equal)
+        vts(C("e0"), C("dlt"), 0.0, None, ALU.is_equal, w=[d_])
+        vts(C("e1"), C("dlt"), 1.0, None, ALU.is_equal)
+        e_ = vts(C("em"), C("dlt"), -1.0, None, ALU.is_equal)
+        c_1 = vtt(C("cb1"), C("e0"), C("e1"), ALU.subtract, w=[e_])
+        c_x = vtt(C("e1"), C("e0"), C("em"), ALU.subtract, w=[c_1])
+        c_2 = vtt(C("cd1"), C("cb1"), C("e1"), ALU.add, w=[c_x])
+        c_3 = vms(C("cd1", 16, 0, 16), 1.0, w=[c_2])
+        c_cd = vtt(C("cd2"), C("cd1"), C("tri"), ALU.mult, w=[c_3])
+        c_zs = vts(T.zs[:, 7:135:8], C("i16", 128, 0, 16), cst[:, 1:2], None, ALU.is_equal, w=[c_zs])
+        t_g = vts(T.gge[:], T.idxa[:], cst[:, 2:3], None, ALU.is_ge, w=[IA, c_th])
+        mm(T.pd[:, 0:256], C("k1", 1), T.zo[0:1, 1, :], True, False, w=[c_k1])
+        mm(T.pd[:, 0:256], C("cd2"), T.gge[:], False, False, w=[c_cd, t_g])
+        need("v", t_g)
+        t_s = do("v", V.tensor_tensor_scan, T.sx[:, 1:257], T.zo[:, 0, :], T.gge[:], 0.0, ALU.add, ALU.add)
+        m_d = mm(T.pd[:, 0:256], C("cd1"), T.sx[:, 0:256], False, True, w=[t_s, c_sx0])
+        c_cb = vtt(C("cb2"), C("cb1"), C("tri"), ALU.mult)
+        hb = [q for q in (rank - 1, rank, rank + 1) if 0 <= q < NR]
+        nc = 8 * len(hb)
+        ca = 8 * hb[0]
+        t1 = vts(T.ei[:, 0, 0:nc], T.endw[:, ca:ca + nc], -4096.0 * rank, 0.0, ALU.add, ALU.max, w=[EN])
+        t_id = vcp(T.id16[:], C("rep", 16, 0, 16), w=[rep])
+        t2 = vts(T.ei[:, 1, 0:nc], T.ei[:, 0, 0:nc], 4096.0, None, ALU.min, w=[t1])
+        t3 = vts(T.ei[:, 2, 0:nc], T.ei[:, 1, 0:nc], 15, None, ALU.bitwise_and, w=[t2])
+        t4 = vts(T.ei[:, 3, 0:nc], T.ei[:, 1, 0:nc], 4, None, ALU.arith_shift_right)
+        t_rb = vcp(T.rbf[:, 0:nc], T.ei[:, 2, 0:nc], w=[t3])
+        t_gd = vtt(T.gd[:], T.pd[:, 0:256], T.gge[:], ALU.mult, w=[m_d])
+        t_cb = vcp(T.cbf[:, 0:nc], T.ei[:, 3, 0:nc], w=[t4])
+        whi, tb, mb = T.col[:, 0, :], T.col[:, 1, :], T.col[:, 2, :]
+        p1 = vts(T.pv[:], T.idxe[:], 8191, None, ALU.bitwise_and, w=[IE])
+        p2 = vts(T.pay[:, 0, :], T.pv[:], -1.0, 8192.0, ALU.mult, ALU.add, w=[p1])
+        p3 = vcp(whi, T.pay[:, 0, :], w=[p2])
+        p4 = vtt(T.pay[:, 1, :], T.pay[:, 0, :], whi, ALU.subtract, w=[p3])
+        for k in range(16):
+            t_dg = act(T.rdg[:, 0:nc, k], T.rbf[:, 0:nc], ACT.Copy, w=[t_rb, t_id], scale=T.id16[:, k:k + 1])
+        m_p = mm(T.pp[:, 0:256], C("cb2"), T.gge[:], True, False, w=[c_cb])
+        m_p = mm(T.pp[:, 0:256], C("cb1"), T.sx[:, 0:256], False, True)
+        for k in range(8):
+            m_a = mm(T.pa[:, 0:32], T.zs[:, 7 - k:135 - k], T.gd[:, 32 * k:32 * k + 32], k == 0, k == 7, w=[t_gd, c_zs])
+        m_c = mm(T.pn[:, 0:nc], C("rep", 16), T.cbf[:, 0:nc], True, True, w=[t_cb])
+        m_r = mm(T.pr[:, 0:16 * nc], T.zo[0:16, 1, 0:128], T.rdg[:, 0:nc, :], True, True, w=[t_dg])
+        need("v", p3)
+        p5 = do("v", V.reciprocal, T.pay[:, 2, :], whi)
+        p6 = vtt(T.pay[:, 3, :], T.pay[:, 1, :], T.pay[:, 2, :], ALU.mult, w=[p5, p4])
+        a1 = vts(T.ti[:], T.pa[:, 0:32], 1.0 / 128, -0.496, ALU.mult, ALU.add, w=[m_a])
+        a2 = vts(tb, T.ti[:], -128.0, None, ALU.mult, w=[a1])
+        a3 = vtt(mb, T.pa[:, 0:32], tb, ALU.add, w=[a2])
+        s_pc = act(T.pc[:, 0:256], T.pp[:, 0:256], ACT.Copy, w=[m_p])
+        s_m0 = act(T.msk[:, 0, 0:16 * nc], T.pr[:, 0:16 * nc], ACT.Abs, w=[m_r, c_nr], bias=cst[:, 3:4])
+        s_mk = act(T.msk[:, 1, 0:16 * nc], T.msk[:, 0, 0:16 * nc], ACT.Relu, w=[s_m0], bias=1.0, scale=-1.0)
+        lag = []
+
+        def low_mm(j, stop):
+            return mm(T.px[:, 0:64], T.oa[:, j, :], T.ob2[:, j, :], False, stop, w=[lag[j]])
+        for k in range(32):
+            vts(T.oa[:, k, :], C("iota_a"), T.col[:, 2, k:k + 1], None, ALU.is_equal, w=[a3, g_ia])
+            o_b = vts(T.ob1[:, k, :], T.iota_b[:], T.col[:, 1, k:k + 1], T.col[:, 0, k:k + 1], ALU.is_equal, ALU.mult, w=[g_ib, p3])
+            lag.append(act(T.ob2[:, k, :], T.ob1[:, k, :], ACT.Copy, w=[o_b, p6], scale=T.pay[:, 3, k:k + 1]))
+            mm(T.px[:, 0:64], T.oa[:, k, :], T.ob1[:, k, :], k == 0, False, w=[o_b])
+            if k >= 3:
+                low_mm(k - 3, False)
+            if k == 3:
+                t_co = vcp(T.cof[:, 0:nc], T.pn[:, 0:nc], w=[m_c])
+                t_p2 = vms(T.pc[:, 256:272], 1024.0)
+                t_os = vts(T.osel[:], T.kc[:, KC.index("cdv"), 0:128:16], cst[:, 0:1], 0.0, ALU.add, ALU.is_equal)
+                t_ms = vms(T.msg[:], 0.0)
+            if k == 15:
+                t_mg = vtt(T.mg[:, 0:16 * nc], T.pc[:].indirect(T.cof[:, 0:nc]), T.msk[:, 1, 0:16 * nc], ALU.mult,
+                           w=[t_co, t_p2, s_pc, s_mk])
+            if k == 24:
+                for j in range(len(hb)):
+                    m_n = mm(T.pn[:, 128 + 8 * j:136 + 8 * j], T.mg[:, 128 * j:128 * j + 128], T.osel[:], True, True, w=[t_mg, t_os, t_co])
+        for j in range(29, 32):
+            m_x = low_mm(j, j == 31)
+        for j, q in enumerate(hb):
+            s_ms = act(T.msg[:, :, 8 + q - rank + 1], T.pn[:, 128 + 8 * j:136 + 8 * j], ACT.Copy, w=[m_n, t_ms])
+        t_ef = vcp(T.ef[:], T.endw[:, 8 * rank - 1:8 * rank + 8]) if rank > 0 else vcp(T.ef[:, 1:9], T.endw[:, 0:8])
+        t_of = vms(T.onef[:], 1.0)
+        z_m = vms(T.zsb[:, 0:16], 0.0)
+        t_mx = vcp(T.msg[:, :, 0:8], T.px[:, 0:64], w=[m_x, t_ms])
+        tr = []
+        tg = [p for p in parts if p[2] <= rank < p[3] and p[0] != core]
+        tg.sort(key=lambda p: len(bits(topo.mask(core, p[0]))))
+        free = bits(topo.mask(core, tg[0][0]))
+        for p in tg:
+            e = [x for x in free if x in bits(topo.mask(core, p[0]))][0]
+            free.remove(e)
+            tr.append(RemoteDMATransfer(src=T.msg[:, p[1], :], dst=T.land[:, rank + 1, :], dst_ids=[dst(p[0])],
+                                        dma_engine_mask=emask([e]), remote_sem=T.sem.arl))
+        need("g", t_mx, s_ms)
+        g.remote_dma_fused(tr, local_sem=T.sem.loc)
+        cnt["loc"] += len(tr)
+        local = s0 <= rank < s1
+        if local:
+            t_ld = vcp(T.land[:, rank + 1, :], T.msg[:, own, :], w=[t_mx, s_ms])
+    for k in range(8):
+        t_sw = vts(T.selw[:, k, :], C("dwr"), 16.0 * k, None, ALU.is_equal, w=[g_dw])
+    z0 = vms(T.land[:, 0:s0 + 1, :], 0.0)
+    z1 = vms(T.land[:, s1 + 1:10, :], 0.0)
+    b_m = vts(T.qm[:, 3, 0:nq], T.qm[:, 3, 0:nq], 0.0, 15.0, ALU.max, ALU.add, w=[g_bm])
+    b_w = vts(F("basew"), F("basew"), 0.0, 15.0, ALU.max, ALU.add, w=[g_bw])
+    for k in range(8):
+        t_sp = vts(T.selp[:, k, :], C("dwr"), 16.0 * k - 1.0, None, ALU.is_equal)
+    t_sp = vts(C("selx"), C("dwr"), 127.0, None, ALU.is_equal)
+    t_lc = vms(T.tabx[:, 8192:8208], LOW)
+    t_gc = vms(T.sc[:, 0:16], LOW)
+    t_lt = vms(T.lowt[:, 0:128 * nq], LOW)
+    t_fl = vms(T.flg[:, 0:16 + 1024 * ns], -LOW)
+    if rank is not None:
+        za = 0 if rank > 0 else 1
+        for k in range(16):
+            t_zd = act(T.zdg[:, za:9, k], T.ef[:, za:9], ACT.Copy, w=[t_ef, t_id], scale=T.id16[:, k:k + 1])
+        m_z = mm(T.pr[:, 16 * za:144], T.onef[:], T.zdg[:, za:9, :], True, True, w=[t_zd, t_of, s_m0])
+        s_z = act(T.zsb[:, 16 * za:144], T.pr[:, 16 * za:144], ACT.Copy, w=[m_z, z_m])
+    AR = ("arl", ns - (1 if local else 0))
+    L = T.land
+    lhi, llo, qhi, qlw = T.lhl[:, 0, 0:8 * ns], T.lhl[:, 1, 0:8 * ns], T.qhl[:, 0, 0:nq], T.qhl[:, 1, 0:nq]
+    w1 = vcp(lhi, L[:, s0 + 1:s1 + 1, 0:8], w=[AR, t_ld])
+    w2 = vtt(llo, L[:, s0 + 1:s1 + 1, 0:8], lhi, ALU.subtract, w=[w1])
+    for k in range(8):
+        mm(T.po[:, k:64 * ns:8], T.selw[:, k, :], lhi, True, False, w=[w1, t_sw])
+        m_o = mm(T.po[:, k:64 * ns:8], T.selw[:, k, :], llo, False, True, w=[w2])
+    q1 = vtt(T.qm[:, 0, 0:nq], L[:, qlo:qlo + nq, 10], L[:, qlo + 1:qlo + 1 + nq, 9], ALU.add, w=[z0, z1])
+    q2 = vtt(T.qm[:, 1, 0:nq], T.qm[:, 0, 0:nq], L[:, qlo + 2:qlo + 2 + nq, 8], ALU.add, w=[q1])
+    q3 = vtt(T.qm[:, 2, 0:nq], T.qm[:, 1, 0:nq], T.qm[:, 3, 0:nq], ALU.add, w=[q2, b_m])
+    q4 = vcp(qhi, T.qm[:, 2, 0:nq], w=[q3])
+    q5 = vtt(qlw, T.qm[:, 2, 0:nq], qhi, ALU.subtract, w=[q4])
+    w3 = vts(T.offs[:, 0:64 * ns], T.po[:, 0:64 * ns], -1.0, 8192.0, ALU.mult, ALU.add, w=[m_o])
+    for k in range(8):
+        mm(T.pq[:, k:n8:8], T.selw[:, k, :], qhi, True, False, w=[q4])
+        mm(T.pq[:, k:n8:8], T.selw[:, k, :], qlw, False, True, w=[q5])
+        mm(T.pq[:, 256 + k:256 + n8:8], T.selp[:, k, :], qhi, True, False, w=[t_sp])
+        if k == 0:
+            mm(T.pq[:, 264:256 + n8:8], C("selx"), T.qhl[:, 0, 0:nq - 1], False, False)
+            mm(T.pq[:, 264:256 + n8:8], C("selx"), T.qhl[:, 1, 0:nq - 1], False, False)
+        m_q = mm(T.pq[:, 256 + k:256 + n8:8], T.selp[:, k, :], qlw, False, True)
+    TAB = [("tb%d" % k, 16) for k in range(4)]
+    if rank is None:
+        TAB = [("taba", 4 * len(table_engines(topo, cores[own], core)))]
+    vset = [k for k in range(ns) if k % 4 == 3]
+    gth = {}
+    for k in range(ns):
+        ind = T.tabx[:].indirect(T.offs[:, 64 * k:64 * k + 64])
+        if k in vset:
+            gth[k] = vcp(T.gt[:, 1024 * k:1024 * k + 1024], ind, w=TAB + [w3, t_lc])
+        else:
+            gth[k] = act(T.gt[:, 1024 * k:1024 * k + 1024], ind, ACT.Copy, w=TAB + [w3, t_lc])
+    f1 = vtt(F("pm"), T.pq[:, 256:256 + n8], F("basew"), ALU.max, w=[m_q, b_w])
+    f2 = vtt(F("ne"), T.pq[:, 0:n8], F("pm"), ALU.is_gt, w=[f1])
+    f3 = vts(F("xx"), F("ne"), -65536.0, None, ALU.mult, w=[f2])
+    f4 = vtt(T.lf[:, 64:64 + n8], T.pq[:, 0:n8], F("ne"), ALU.mult)
+    f5 = vtt(F("x2"), F("xx"), F("trash"), ALU.add, w=[f3, g_tr])
+    f6 = vtt(T.lf[:, 0:n8], F("x2"), F("pm"), ALU.max, w=[f5])
+    f7 = vcp(T.lfu[:, 0:n8], T.lf[:, 0:n8], w=[f6])
+    f8 = vcp(T.lfu[:, 64:64 + n8], T.lf[:, 64:64 + n8], w=[f4])
+    fw = 16 + 1024 * ns + 1136
+    fl = vcp(T.flg[:, 0:fw].indirect(T.lfu[:, 0:n8]), T.lowt[:, 0:128 * nq], w=[f7, t_fl, t_lt])
+    if rank is not None:
+        z_q = vtt(C("zt"), T.zsb[:, 16:144], T.zsb[:, 15:143], ALU.is_equal, w=[s_z])
+        z_z = vts(C("zz"), C("zt"), -1.0, -LOW, ALU.add, ALU.mult, w=[z_q])
+    scn = []
+    for k in range(ns):
+        ini = LOW if k == 0 else T.sc[:, 15 + 1024 * k:16 + 1024 * k]
+        need("v", gth[k], fl, scn[k - 1] if k else t_gc)
+        scn.append(do("v", V.tensor_tensor_scan, T.sc[:, 16 + 1024 * k:1040 + 1024 * k], T.flg[:, 15 + 1024 * k:1039 + 1024 * k],
+                      T.gt[:, 1024 * k:1024 * k + 1024], ini, ALU.min, ALU.max))
+    done = {}
+    gl = groups(part)
+    for gi, grp in enumerate(gl):
+        es = engines(topo, cores, part, grp)
+        order = [q for q in grp if q in es] + [q for q in grp if q not in es]
+        for n, q in enumerate(order):
+            qi = q - qlo
+            k = ready(part, q)
+            win = T.sc[:, 0:1040 + 1024 * k].indirect(T.lfu[:, 64 + 8 * qi:72 + 8 * qi])
+            if gi == len(gl) - 1 and n % 2 == 0:
+                done[q] = vcp(T.part[:, qi, :], win, w=[scn[k], f8])
+            else:
+                done[q] = act(T.part[:, qi, :], win, ACT.Copy, w=[scn[k], f8])
+        tr = []
+        for q in grp:
+            if q in es:
+                sl = [p[0] for p in parts if q in p[4]].index(core)
+                tr.append(RemoteDMATransfer(src=T.part[:, q - qlo, :], dst=T.pland[:, sl, :], dst_ids=[dst(cores[q])],
+                                            dma_engine_mask=emask(es[q]), remote_sem=T.sem["pa%d" % sl]))
+        if tr:
+            need("g", *[done[q] for q in es])
+            g.remote_dma_fused(tr, local_sem=T.sem.loc)
+            cnt["loc"] += sum(len(es[q]) for q in es)
+    if rank is not None:
+        arr = []
+        for i, p in enumerate([p for p in parts if rank in p[4]]):
+            gi = [j for j, x in enumerate(groups(p)) if rank in x][0]
+            if p[0] == core:
+                arr.append((gi, -1, T.part[:, rank - qlo, :], done[rank]))
+            else:
+                arr.append((gi, i, T.pland[:, i, :], ("pa%d" % i, len(engines(topo, cores, p, groups(p)[gi])[rank]))))
+        arr.sort(key=lambda x: x[0:2])
+        acc, tok = C("zz"), z_z
+        for i, (_, _, ap, w) in enumerate(arr):
+            out = T.ysb[:] if i == len(arr) - 1 else T.pd[:, 0:128]
+            tok = vtt(out, acc, ap, ALU.max, w=[tok, w, m_d])
+            acc = out
+        need("y", tok)
+        g.sync.dma_start(T.y[:], T.ysb[:]).then_inc(T.sem.yd, 16)
+        need("y", ("yd", 16))
+    need("g", *[(k, cnt[k]) for k in cnt])

@@ -2,16 +2,21 @@ from concourse.bass import DstId, RemoteDMATransfer
 from concourse.mybir import AluOpType as ALU, ActivationFunctionType as ACT
 NR = 8
 HS = 4
+VB = [k for k in range(32) if k % 4 == 1]
+LAG = 4
+NB = 3
+LAY = (0, 1, 1, 0)
 LOW = -201.0 * 2.0 ** 92
 NCORES = 128
-KC = ["i16", "cdv", "iota_a", "dwr", "dlt", "e0", "e1", "em", "tri", "rep", "cb1", "cb2", "cd1", "cd2", "k1", "selx", "zt", "zz"]
-KF = ["basew", "trash", "pm", "ne", "xx", "x2"]
+KC = ["i16", "cdv", "iota_a", "dwr", "dlt", "e0", "e1", "tri", "rep", "cd1", "cd2", "k1", "selx", "zt", "zz"]
+KF = ["basew", "trash", "pm", "ee", "xx", "qq", "x2"]
 SPEC = {
-    "float32": "cst 8,kf 6 64,pc 272,zsb 144,pay 4 32,msg 8 12,land 10 12,qm 4 8,lf 128",
-    "bfloat16": "kc 18 128,tabx 8208,iota_b 64,zo 2 256,zs 136,osel 8,selw 8 128,selp 8 128,gge 256,sx 272,msk 2 384,col 3 32,"
-                "oa 32 128,ob1 32 64,ob2 32 64,lhl 2 64,qhl 2 8,flg 9344,lowt 1024,gt 8192,sc 8208,part 8 128,pland 16 128,ysb 128",
-    "int32": "idxa 256,idxe 32,pidx 4,pv 32,ti 32", "float16": "gd 256,mg 384", "uint16": "cof 32,offs 512,lfu 128"}
-SCRATCH = {}
+    "float32": "cst 8,kf 7 64,hsm 2 64,pc 272,zsb 144,pay 4 32,msg 8 12,land 10 12,qm 4 8,lf 128",
+    "bfloat16": "kc 15 128,tabx 8208,iota_b 64,zo 2 256,zs 136,osel 8,selw 8 128,selp 8 128,gge 256,sx 272,msk 384,col 4 32,"
+                "oa 32 128,ob1 32 64,ob2 32 64,lhl 2 64,qhl 2 8,flg 9344,lowt 1024,gt 8192,sc 8208,part 8 128,"
+                "pland 17 128,ysb 128",
+    "int32": "idxa 256,idxe 32,pidx 4,pv 32,ti 32,e8 8", "float16": "gd 256,mg 384", "uint16": "cof 32,offs 512,lfu 128"}
+SCRATCH = {"ehd": ("dram", [128, 8], "int32")}
 for _dt in SPEC:
     for _e in SPEC[_dt].split(","):
         _w = _e.split()
@@ -20,9 +25,11 @@ for _n, _sh, _dt in (("endw", [16, 64], "int32"), ("onef", [16, 128], "float32")
                      ("ei", [16, 4, 32], "int32"), ("cbf", [16, 24], "bfloat16"), ("rbf", [16, 24], "bfloat16"),
                      ("rdg", [16, 24, 16], "bfloat16"), ("ef", [16, 9], "float32"), ("zdg", [16, 9, 16], "float32")):
     SCRATCH[_n] = ("sbuf", _sh, _dt)
-for _n in ("pd", "pp", "pa", "pr", "px", "pn", "po", "pq"):
+for _n in ("pd", "pp", "pa", "pr", "px", "pn", "po"):
     SCRATCH[_n] = ("psum", [128, 512], "float32")
-SEMAPHORES = ["v", "s", "p", "gi", "ia", "ie", "en", "tb0", "tb1", "tb2", "tb3", "yd", "arl", "loc", "taba"] + ["pa%d" % i for i in range(16)]
+SCRATCH["pq"] = ("psum", [128, 2, 256], "float32")
+SEMAPHORES = ["v", "s", "p", "gi", "ia", "ie", "en", "e8d", "eh", "zl", "tb0", "tb1", "tb2", "tb3", "yd", "arl", "loc", "taba"] \
+    + ["pa%d" % i for i in range(16)]
 
 
 def bits(m):
@@ -33,16 +40,28 @@ def emask(es):
     return sum(1 << e for e in es)
 
 
+def pool(topo, cores, c):
+    es = list(range(16))
+    for d in cores:
+        if d != c:
+            es = [e for e in es if e in bits(topo.mask(c, d))]
+    return es
+
+
+def table_engines(topo, cores, a, b, k):
+    es = pool(topo, cores, a)
+    return [e for e in bits(topo.mask(a, b)) if e not in es] if LAY[k] else es
+
+
 def plan(T, topo):
     cores = list(T.cores)
     parts = [(cores[o], o, 0, HS) for o in range(NR)]
     used = []
-    if HS < NR:
-        for o in range(NR):
-            h = [c for c in range(NCORES) if topo.chip(c) == topo.chip(cores[o]) and c not in cores and c not in used
-                 and all(topo.may_write(c, d) for d in cores)][0]
-            used.append(h)
-            parts.append((h, o, HS, NR))
+    for o in range(NR):
+        h = [c for c in range(NCORES) if topo.chip(c) == topo.chip(cores[o]) and c not in cores and c not in used
+             and all(topo.may_write(c, d) for d in cores)][0]
+        used.append(h)
+        parts.append((h, o, HS, NR))
     return [p + ([q for q in range(NR) if q + 1 >= p[2] and q - 1 < p[3]],) for p in parts]
 
 
@@ -51,9 +70,9 @@ def ready(part, q):
 
 
 def groups(part):
-    ns = part[3] - part[2]
-    a = [q for q in part[4] if ready(part, q) < ns - 1]
-    b = [q for q in part[4] if ready(part, q) == ns - 1]
+    lim = part[3] - part[2] - (1 if part[2] == 0 else 2)
+    a = [q for q in part[4] if ready(part, q) < lim]
+    b = [q for q in part[4] if ready(part, q) >= lim]
     return [x for x in (a, b) if x]
 
 
@@ -61,18 +80,11 @@ def engines(topo, cores, part, grp):
     dst = [q for q in grp if cores[q] != part[0]]
     if not dst:
         return {}
-    pool = bits(topo.mask(part[0], cores[dst[0]]))
-    for q in dst:
-        pool = [e for e in pool if e in bits(topo.mask(part[0], cores[q]))]
+    es = pool(topo, cores, part[0])
     n = 1
-    while 2 * n * len(dst) <= min(len(pool), 8):
+    while 2 * n * len(dst) <= len(es):
         n *= 2
-    return {q: pool[n * i:n * i + n] for i, q in enumerate(dst)}
-
-
-def table_engines(topo, a, b):
-    hm = bits(topo.mask(a, b))
-    return hm[len(hm) // 2:]
+    return {q: es[n * i:n * i + n] for i, q in enumerate(dst)}
 
 
 def rank_program(g, core, T, topo):
@@ -140,6 +152,11 @@ def rank_program(g, core, T, topo):
             return do("g", g.iota, out, pat, base, cm, allow_small_or_imprecise_dtypes=True)
         return do("g", g.iota, out, pat, base, cm)
 
+    def rdma(c, out, in_, sem, es):
+        a = topo.addr(c)
+        g.remote_dma(out, in_, T.sem[sem], T.sem.loc, a[1], a[0], emask(es))
+        cnt["loc"] += len(es)
+
     def dst(c):
         a = topo.addr(c)
         return DstId(rid=a[0], pnc=a[1])
@@ -150,147 +167,148 @@ def rank_program(g, core, T, topo):
     def F(n):
         return T.kf[:, KF.index(n), 0:n8]
 
-    helper = [p[0] for p in parts if p[1] == own and p[0] != core and rank is not None]
+    mate = [p[0] for p in parts if p[1] == own and p[0] != core][0]
+    es8 = pool(topo, cores, core)
     IA, IE, EN = ("ia", 128), ("ie", 16), ("en", 16)
     if rank is not None:
+        g.sync.dma_start(T.e8[:], T.end[:]).then_inc(T.sem.e8d, 16)
+        g.scalar.dma_start(T.endw[:], T.end[:]).then_inc(T.sem.en, 16)
         for o in range(4):
             g.sync.dma_start(T.idxa[16 * o:16 * o + 16, :], T.idx[:]).then_inc(T.sem.ia, 16)
             g.scalar.dma_start(T.idxa[64 + 16 * o:80 + 16 * o, :], T.idx[:]).then_inc(T.sem.ia, 16)
-        g.scalar.dma_start(T.endw[:], T.end[:]).then_inc(T.sem.en, 16)
         g.sync.dma_start(T.idxe[:], T.idx[:]).then_inc(T.sem.ie, 16)
         for k in range(4):
             g.sync.dma_start(T.tabx[:, 2048 * k:2048 * k + 2048], T.tab[:, 2048 * k:2048 * k + 2048]).then_inc(T.sem["tb%d" % k], 16)
+    else:
+        need("y", ("eh", len(pool(topo, cores, mate))))
+        g.sync.dma_start(T.endw[:], T.ehd[:]).then_inc(T.sem.en, 16)
     pidx, cst = T.pidx, T.cst
+    g_pi = iota(pidx[:, 0:1], [[0, 1]], 0, 1, False)
     if rank is not None:
-        g_pi = iota(pidx[:, 0:1], [[0, 1]], 0, 1, False)
-        g_16 = iota(C("i16"), [[0, 8], [1, 16]], 0, 0)
         g_cd = iota(C("cdv"), [[-1, 8], [0, 16]], 0, 0)
+    g_16 = iota(C("i16"), [[0, 8], [1, 16]], 0, 0)
+    if rank is not None:
         g_ia = iota(C("iota_a"), [[1, 128]], 0, 0)
         g_ib = iota(T.iota_b[:], [[-128, 64]], 0, 0)
+        need("g", ("e8d", 16))
+        rdma(mate, T.ehd[:], T.e8[:], "eh", es8)
     g_dw = iota(C("dwr"), [[0, 8], [-1, 16]], 0, 1)
     g_bm = iota(T.qm[:, 3, 0:nq], [[1024, nq]], 1024 * (qlo - 1 - s0), 0)
     g_bw = iota(F("basew"), [[1024, nq], [0, 8]], 1024 * (qlo - 1 - s0), 0)
     g_tr = iota(F("trash"), [[16, n8]], 16 + 1024 * ns, 1)
-    t_ef = t_id = None
     local, t_ld = False, None
+    t_fs = None
+
+    def table_on(k):
+        need("g", ("tb%d" % k, 16))
+        rdma(mate, T.tabx[:, 2048 * k:2048 * k + 2048], T.tabx[:, 2048 * k:2048 * k + 2048], "taba",
+             table_engines(topo, cores, core, mate, k))
+    ri = vts(pidx[:, 2:3], pidx[:, 0:1], 15, None, ALU.bitwise_and, w=[g_pi])
     if rank is not None:
-        if helper:
-            hm = table_engines(topo, core, helper[0])
-            for k in range(4):
-                need("g", ("tb%d" % k, 16))
-                a = topo.addr(helper[0])
-                g.remote_dma(T.tabx[:, 2048 * k:2048 * k + 2048], T.tabx[:, 2048 * k:2048 * k + 2048], T.sem.taba, T.sem.loc,
-                             a[1], a[0], emask(hm))
-                cnt["loc"] += len(hm)
-        oi = vts(pidx[:, 1:2], pidx[:, 0:1], 4, None, ALU.arith_shift_right, w=[g_pi])
-        ri = vts(pidx[:, 2:3], pidx[:, 0:1], 15, None, ALU.bitwise_and)
-        vms(T.zo[:, 0, :], 0.0)
-        vms(T.zo[:, 1, :], 1.0)
-        c_sx0 = vms(T.sx[:, 0:1], 0.0)
-        c_of = vcp(cst[:, 0:1], pidx[:, 1:2], w=[oi])
-        c_th = vts(cst[:, 2:3], pidx[:, 1:2], 8192.0, None, ALU.mult)
-        c_rf = vcp(cst[:, 1:2], pidx[:, 2:3], w=[ri])
-        c_nr = vts(cst[:, 3:4], pidx[:, 2:3], -1.0, None, ALU.mult)
-        c_zs = vms(T.zs[:], 0.0)
-        vms(C("k1", 1, 0, 16), 0.0)
-        c_k1 = vms(C("k1", 1, 16, 128), 1024.0)
-        d_ = vts(C("dlt"), C("cdv"), cst[:, 0:1], None, ALU.add, w=[g_cd, c_of])
-        vts(C("tri"), C("i16"), cst[:, 1:2], None, ALU.is_gt, w=[g_16, c_rf])
-        rep = vts(C("rep"), C("i16"), cst[:, 1:2], None, ALU.is_equal)
-        vts(C("e0"), C("dlt"), 0.0, None, ALU.is_equal, w=[d_])
-        vts(C("e1"), C("dlt"), 1.0, None, ALU.is_equal)
-        e_ = vts(C("em"), C("dlt"), -1.0, None, ALU.is_equal)
-        c_1 = vtt(C("cb1"), C("e0"), C("e1"), ALU.subtract, w=[e_])
-        c_x = vtt(C("e1"), C("e0"), C("em"), ALU.subtract, w=[c_1])
-        c_2 = vtt(C("cd1"), C("cb1"), C("e1"), ALU.add, w=[c_x])
-        c_3 = vms(C("cd1", 16, 0, 16), 1.0, w=[c_2])
-        c_cd = vtt(C("cd2"), C("cd1"), C("tri"), ALU.mult, w=[c_3])
-        c_zs = vts(T.zs[:, 7:135:8], C("i16", 128, 0, 16), cst[:, 1:2], None, ALU.is_equal, w=[c_zs])
-        t_g = vts(T.gge[:], T.idxa[:], cst[:, 2:3], None, ALU.is_ge, w=[IA, c_th])
-        mm(T.pd[:, 0:256], C("k1", 1), T.zo[0:1, 1, :], True, False, w=[c_k1])
-        mm(T.pd[:, 0:256], C("cd2"), T.gge[:], False, False, w=[c_cd, t_g])
-        need("v", t_g)
-        t_s = do("v", V.tensor_tensor_scan, T.sx[:, 1:257], T.zo[:, 0, :], T.gge[:], 0.0, ALU.add, ALU.add)
-        m_d = mm(T.pd[:, 0:256], C("cd1"), T.sx[:, 0:256], False, True, w=[t_s, c_sx0])
-        c_cb = vtt(C("cb2"), C("cb1"), C("tri"), ALU.mult)
+        for k in range(NB):
+            table_on(k)
         hb = [q for q in (rank - 1, rank, rank + 1) if 0 <= q < NR]
         nc = 8 * len(hb)
         ca = 8 * hb[0]
-        t1 = vts(T.ei[:, 0, 0:nc], T.endw[:, ca:ca + nc], -4096.0 * rank, 0.0, ALU.add, ALU.max, w=[EN])
+        oi = vts(pidx[:, 1:2], pidx[:, 0:1], 4, None, ALU.arith_shift_right)
+        vms(C("k1", 1, 0, 16), 0.0)
+        c_rf = vcp(cst[:, 1:2], pidx[:, 2:3], w=[ri])
+        c_of = vcp(cst[:, 0:1], pidx[:, 1:2], w=[oi])
+        c_k1 = vms(C("k1", 1, 16, 128), 1024.0)
+        c_th = vts(cst[:, 2:3], pidx[:, 1:2], 8192.0, None, ALU.mult)
+        c_c0 = vts(cst[:, 4:5], pidx[:, 1:2], 0.0, 1024.0, ALU.is_equal, ALU.mult)
+        vms(T.zo[:, 0, :], 0.0)
+        c_nb = vts(cst[:, 5:6], cst[:, 4:5], -1024.0, None, ALU.add, w=[c_c0])
+        s_ab = act(C("dlt"), C("cdv"), ACT.Abs, w=[g_cd, c_of], bias=cst[:, 0:1])
+        c_zo = vms(T.zo[:, 1, :], 1.0)
+        c_sx0 = vms(T.sx[:, 0:1], 0.0)
+        vts(C("tri"), C("i16"), cst[:, 1:2], None, ALU.is_gt, w=[g_16, c_rf])
+        rep = vts(C("rep"), C("i16"), cst[:, 1:2], None, ALU.is_equal)
+        vts(C("e0"), C("dlt"), 0.0, 2.0, ALU.is_equal, ALU.mult, w=[s_ab])
+        e_ = vts(C("e1"), C("dlt"), 1.0, -1.0, ALU.is_equal, ALU.mult)
         t_id = vcp(T.id16[:], C("rep", 16, 0, 16), w=[rep])
+        c_2 = vtt(C("cd1"), C("e0"), C("e1"), ALU.add, w=[e_])
+        t1 = vts(T.ei[:, 0, 0:nc], T.endw[:, ca:ca + nc], -4096.0 * rank, 0.0, ALU.add, ALU.max, w=[EN])
+        c_3 = vms(C("cd1", 16, 0, 16), 1.0, w=[c_2])
         t2 = vts(T.ei[:, 1, 0:nc], T.ei[:, 0, 0:nc], 4096.0, None, ALU.min, w=[t1])
+        c_cd = vtt(C("cd2"), C("cd1"), C("tri"), ALU.mult, w=[c_3])
         t3 = vts(T.ei[:, 2, 0:nc], T.ei[:, 1, 0:nc], 15, None, ALU.bitwise_and, w=[t2])
-        t4 = vts(T.ei[:, 3, 0:nc], T.ei[:, 1, 0:nc], 4, None, ALU.arith_shift_right)
+        c_zs = vms(T.zs[:], 0.0)
         t_rb = vcp(T.rbf[:, 0:nc], T.ei[:, 2, 0:nc], w=[t3])
-        t_gd = vtt(T.gd[:], T.pd[:, 0:256], T.gge[:], ALU.mult, w=[m_d])
-        t_cb = vcp(T.cbf[:, 0:nc], T.ei[:, 3, 0:nc], w=[t4])
-        whi, tb, mb = T.col[:, 0, :], T.col[:, 1, :], T.col[:, 2, :]
-        p1 = vts(T.pv[:], T.idxe[:], 8191, None, ALU.bitwise_and, w=[IE])
-        p2 = vts(T.pay[:, 0, :], T.pv[:], -1.0, 8192.0, ALU.mult, ALU.add, w=[p1])
-        p3 = vcp(whi, T.pay[:, 0, :], w=[p2])
-        p4 = vtt(T.pay[:, 1, :], T.pay[:, 0, :], whi, ALU.subtract, w=[p3])
+        t_g = vts(T.gge[:], T.idxa[:], cst[:, 2:3], None, ALU.is_ge, w=[IA, c_th])
+        mm(T.pd[:, 0:256], C("k1", 1), T.zo[0:1, 1, :], True, False, w=[c_k1, c_zo])
+        mm(T.pd[:, 0:256], C("cd2"), T.gge[:], False, False, w=[c_cd, t_g])
+        need("v", t_g, c_zo)
+        t_s = do("v", V.tensor_tensor_scan, T.sx[:, 1:257], T.zo[:, 0, :], T.gge[:], 0.0, ALU.add, ALU.add)
+        m_d = mm(T.pd[:, 0:256], C("cd1"), T.sx[:, 0:256], False, True, w=[t_s, c_sx0])
         for k in range(16):
             t_dg = act(T.rdg[:, 0:nc, k], T.rbf[:, 0:nc], ACT.Copy, w=[t_rb, t_id], scale=T.id16[:, k:k + 1])
-        m_p = mm(T.pp[:, 0:256], C("cb2"), T.gge[:], True, False, w=[c_cb])
-        m_p = mm(T.pp[:, 0:256], C("cb1"), T.sx[:, 0:256], False, True)
+        c_zs = vts(T.zs[:, 7:135:8], C("i16", 128, 0, 16), cst[:, 1:2], None, ALU.is_equal, w=[c_zs])
+        t4 = vts(T.ei[:, 3, 0:nc], T.ei[:, 1, 0:nc], 4, None, ALU.arith_shift_right, w=[t2])
+        whi, tb, mb = T.col[:, 0, :], T.col[:, 1, :], T.col[:, 2, :]
+        p1 = vts(T.pv[:], T.idxe[:], 8191, None, ALU.bitwise_and, w=[IE])
+        t_gd = vtt(T.gd[:], T.pd[:, 0:256], T.gge[:], ALU.mult, w=[m_d])
+        p2 = vts(T.pay[:, 0, :], T.pv[:], -1.0, 8192.0, ALU.mult, ALU.add, w=[p1])
+        t_cb = vcp(T.cbf[:, 0:nc], T.ei[:, 3, 0:nc], w=[t4])
+        p3 = vcp(whi, T.pay[:, 0, :], w=[p2])
+        p4 = vtt(T.col[:, 3, :], T.pay[:, 0, :], whi, ALU.subtract, w=[p3])
+        p5 = do("v", V.reciprocal, T.pay[:, 2, :], whi)
+        p6 = vtt(T.pay[:, 3, :], T.col[:, 3, :], T.pay[:, 2, :], ALU.mult, w=[p5, p4])
         for k in range(8):
             m_a = mm(T.pa[:, 0:32], T.zs[:, 7 - k:135 - k], T.gd[:, 32 * k:32 * k + 32], k == 0, k == 7, w=[t_gd, c_zs])
-        m_c = mm(T.pn[:, 0:nc], C("rep", 16), T.cbf[:, 0:nc], True, True, w=[t_cb])
         m_r = mm(T.pr[:, 0:16 * nc], T.zo[0:16, 1, 0:128], T.rdg[:, 0:nc, :], True, True, w=[t_dg])
-        need("v", p3)
-        p5 = do("v", V.reciprocal, T.pay[:, 2, :], whi)
-        p6 = vtt(T.pay[:, 3, :], T.pay[:, 1, :], T.pay[:, 2, :], ALU.mult, w=[p5, p4])
+        m_c = mm(T.pn[:, 0:nc], C("rep", 16), T.cbf[:, 0:nc], True, True, w=[t_cb])
+        s_pc = act(T.pc[:, 0:256], T.pd[:, 0:256], ACT.Identity, w=[m_d, t_gd, c_nb], bias=cst[:, 5:6])
         a1 = vts(T.ti[:], T.pa[:, 0:32], 1.0 / 128, -0.496, ALU.mult, ALU.add, w=[m_a])
         a2 = vts(tb, T.ti[:], -128.0, None, ALU.mult, w=[a1])
         a3 = vtt(mb, T.pa[:, 0:32], tb, ALU.add, w=[a2])
-        s_pc = act(T.pc[:, 0:256], T.pp[:, 0:256], ACT.Copy, w=[m_p])
-        s_m0 = act(T.msk[:, 0, 0:16 * nc], T.pr[:, 0:16 * nc], ACT.Abs, w=[m_r, c_nr], bias=cst[:, 3:4])
-        s_mk = act(T.msk[:, 1, 0:16 * nc], T.msk[:, 0, 0:16 * nc], ACT.Relu, w=[s_m0], bias=1.0, scale=-1.0)
-        lag = []
+        lag = {}
 
         def low_mm(j, stop):
             return mm(T.px[:, 0:64], T.oa[:, j, :], T.ob2[:, j, :], False, stop, w=[lag[j]])
         for k in range(32):
             vts(T.oa[:, k, :], C("iota_a"), T.col[:, 2, k:k + 1], None, ALU.is_equal, w=[a3, g_ia])
             o_b = vts(T.ob1[:, k, :], T.iota_b[:], T.col[:, 1, k:k + 1], T.col[:, 0, k:k + 1], ALU.is_equal, ALU.mult, w=[g_ib, p3])
-            lag.append(act(T.ob2[:, k, :], T.ob1[:, k, :], ACT.Copy, w=[o_b, p6], scale=T.pay[:, 3, k:k + 1]))
+            if k in VB:
+                lag[k] = vts(T.ob2[:, k, :], T.iota_b[:], T.col[:, 1, k:k + 1], T.col[:, 3, k:k + 1], ALU.is_equal, ALU.mult, w=[p4])
+            else:
+                lag[k] = act(T.ob2[:, k, :], T.ob1[:, k, :], ACT.Copy, w=[o_b, p6], scale=T.pay[:, 3, k:k + 1])
             mm(T.px[:, 0:64], T.oa[:, k, :], T.ob1[:, k, :], k == 0, False, w=[o_b])
-            if k >= 3:
-                low_mm(k - 3, False)
-            if k == 3:
+            if k >= LAG:
+                low_mm(k - LAG, False)
+            if k == 5:
                 t_co = vcp(T.cof[:, 0:nc], T.pn[:, 0:nc], w=[m_c])
-                t_p2 = vms(T.pc[:, 256:272], 1024.0)
-                t_os = vts(T.osel[:], T.kc[:, KC.index("cdv"), 0:128:16], cst[:, 0:1], 0.0, ALU.add, ALU.is_equal)
+                t_p2 = vts(T.pc[:, 256:272], T.zo[:, 1, 0:16], cst[:, 4:5], None, ALU.mult)
+                t_os = vts(T.osel[:], T.kc[:, KC.index("cdv"), 0:128:16], cst[:, 0:1], 0.0, ALU.add, ALU.is_le)
                 t_ms = vms(T.msg[:], 0.0)
-            if k == 15:
-                t_mg = vtt(T.mg[:, 0:16 * nc], T.pc[:].indirect(T.cof[:, 0:nc]), T.msk[:, 1, 0:16 * nc], ALU.mult,
-                           w=[t_co, t_p2, s_pc, s_mk])
-            if k == 24:
+            if k == 8:
+                t_mk = vts(T.msk[:, 0:16 * nc], T.pr[:, 0:16 * nc], cst[:, 1:2], None, ALU.is_equal, w=[m_r])
+            if k == 14:
+                t_mg = vtt(T.mg[:, 0:16 * nc], T.pc[:].indirect(T.cof[:, 0:nc]), T.msk[:, 0:16 * nc], ALU.mult,
+                           w=[t_co, t_p2, s_pc, t_mk])
+            if k == 20:
                 for j in range(len(hb)):
                     m_n = mm(T.pn[:, 128 + 8 * j:136 + 8 * j], T.mg[:, 128 * j:128 * j + 128], T.osel[:], True, True, w=[t_mg, t_os, t_co])
-        for j in range(29, 32):
+        for j in range(32 - LAG, 32):
             m_x = low_mm(j, j == 31)
         for j, q in enumerate(hb):
-            s_ms = act(T.msg[:, :, 8 + q - rank + 1], T.pn[:, 128 + 8 * j:136 + 8 * j], ACT.Copy, w=[m_n, t_ms])
-        t_ef = vcp(T.ef[:], T.endw[:, 8 * rank - 1:8 * rank + 8]) if rank > 0 else vcp(T.ef[:, 1:9], T.endw[:, 0:8])
-        t_of = vms(T.onef[:], 1.0)
-        z_m = vms(T.zsb[:, 0:16], 0.0)
-        t_mx = vcp(T.msg[:, :, 0:8], T.px[:, 0:64], w=[m_x, t_ms])
-        tr = []
+            vcp(T.msg[:, :, 8 + q - rank + 1], T.pn[:, 128 + 8 * j:136 + 8 * j], w=[m_n, t_ms])
+        t_mx = vcp(T.msg[:, :, 0:8], T.px[:, 0:64], w=[m_x])
         tg = [p for p in parts if p[2] <= rank < p[3] and p[0] != core]
-        tg.sort(key=lambda p: len(bits(topo.mask(core, p[0]))))
-        free = bits(topo.mask(core, tg[0][0]))
-        for p in tg:
-            e = [x for x in free if x in bits(topo.mask(core, p[0]))][0]
-            free.remove(e)
-            tr.append(RemoteDMATransfer(src=T.msg[:, p[1], :], dst=T.land[:, rank + 1, :], dst_ids=[dst(p[0])],
-                                        dma_engine_mask=emask([e]), remote_sem=T.sem.arl))
-        need("g", t_mx, s_ms)
-        g.remote_dma_fused(tr, local_sem=T.sem.loc)
-        cnt["loc"] += len(tr)
+        need("g", t_mx)
+        g.remote_dma_fused([RemoteDMATransfer(src=T.msg[:, p[1], :], dst=T.land[:, rank + 1, :], dst_ids=[dst(p[0])],
+                                              dma_engine_mask=emask([e]), remote_sem=T.sem.arl) for p, e in zip(tg, es8)],
+                           local_sem=T.sem.loc)
+        cnt["loc"] += len(tg)
+        for k in range(NB, 4):
+            table_on(k)
         local = s0 <= rank < s1
         if local:
-            t_ld = vcp(T.land[:, rank + 1, :], T.msg[:, own, :], w=[t_mx, s_ms])
+            t_ld = vcp(T.land[:, rank + 1, :], T.msg[:, own, :], w=[t_mx])
+        t_fs = act(T.flg[:, 16 + 512 * ns:16 + 1024 * ns], T.oa[:, 0:4 * ns, :], ACT.Identity, w=[t_mx], bias=-LOW, scale=0.0)
+    else:
+        c_rf = vcp(cst[:, 1:2], pidx[:, 2:3], w=[ri])
+        t_id = vts(T.id16[:], C("i16", 16, 0, 16), cst[0:16, 1:2], None, ALU.is_equal, w=[c_rf, g_16])
     for k in range(8):
         t_sw = vts(T.selw[:, k, :], C("dwr"), 16.0 * k, None, ALU.is_equal, w=[g_dw])
     z0 = vms(T.land[:, 0:s0 + 1, :], 0.0)
@@ -303,13 +321,20 @@ def rank_program(g, core, T, topo):
     t_lc = vms(T.tabx[:, 8192:8208], LOW)
     t_gc = vms(T.sc[:, 0:16], LOW)
     t_lt = vms(T.lowt[:, 0:128 * nq], LOW)
-    t_fl = vms(T.flg[:, 0:16 + 1024 * ns], -LOW)
-    if rank is not None:
-        za = 0 if rank > 0 else 1
+    t_fl = vms(T.flg[:, 0:16 + (1024 if t_fs is None else 512) * ns], -LOW)
+    if rank is None:
+        za = 0 if own > 0 else 1
+        t_of = vms(T.onef[:], 1.0)
+        z_m = vms(T.zsb[:, 0:16], 0.0)
+        t_ef = vcp(T.ef[:, za:9], T.endw[:, 8 * own - 1 + za:8 * own + 8], w=[EN])
         for k in range(16):
             t_zd = act(T.zdg[:, za:9, k], T.ef[:, za:9], ACT.Copy, w=[t_ef, t_id], scale=T.id16[:, k:k + 1])
-        m_z = mm(T.pr[:, 16 * za:144], T.onef[:], T.zdg[:, za:9, :], True, True, w=[t_zd, t_of, s_m0])
+        m_z = mm(T.pr[:, 16 * za:144], T.onef[:], T.zdg[:, za:9, :], True, True, w=[t_zd, t_of])
         s_z = act(T.zsb[:, 16 * za:144], T.pr[:, 16 * za:144], ACT.Copy, w=[m_z, z_m])
+        z_q = vtt(C("zt"), T.zsb[:, 16:144], T.zsb[:, 15:143], ALU.is_equal, w=[s_z, z_m])
+        z_z = vts(C("zz"), C("zt"), -1.0, -LOW, ALU.add, ALU.mult, w=[z_q])
+        need("g", z_z)
+        rdma(mate, T.pland[:, 16, :], C("zz"), "zl", es8)
     AR = ("arl", ns - (1 if local else 0))
     L = T.land
     lhi, llo, qhi, qlw = T.lhl[:, 0, 0:8 * ns], T.lhl[:, 1, 0:8 * ns], T.qhl[:, 0, 0:nq], T.qhl[:, 1, 0:nq]
@@ -325,56 +350,53 @@ def rank_program(g, core, T, topo):
     q5 = vtt(qlw, T.qm[:, 2, 0:nq], qhi, ALU.subtract, w=[q4])
     w3 = vts(T.offs[:, 0:64 * ns], T.po[:, 0:64 * ns], -1.0, 8192.0, ALU.mult, ALU.add, w=[m_o])
     for k in range(8):
-        mm(T.pq[:, k:n8:8], T.selw[:, k, :], qhi, True, False, w=[q4])
-        mm(T.pq[:, k:n8:8], T.selw[:, k, :], qlw, False, True, w=[q5])
-        mm(T.pq[:, 256 + k:256 + n8:8], T.selp[:, k, :], qhi, True, False, w=[t_sp])
+        mm(T.pq[:, 0, k:2 * n8:8], T.selw[:, k, :], T.qhl[:, :, 0:nq], True, True, w=[q4, q5])
+        m_q = mm(T.pq[:, 1, k:2 * n8:8], T.selp[:, k, :], T.qhl[:, :, 0:nq], True, k > 0, w=[t_sp])
         if k == 0:
-            mm(T.pq[:, 264:256 + n8:8], C("selx"), T.qhl[:, 0, 0:nq - 1], False, False)
-            mm(T.pq[:, 264:256 + n8:8], C("selx"), T.qhl[:, 1, 0:nq - 1], False, False)
-        m_q = mm(T.pq[:, 256 + k:256 + n8:8], T.selp[:, k, :], qlw, False, True)
+            mm(T.pq[:, 1, 8:n8:8], C("selx"), T.qhl[:, 0, 0:nq - 1], False, False)
+            mm(T.pq[:, 1, n8 + 8:2 * n8:8], C("selx"), T.qhl[:, 1, 0:nq - 1], False, True)
     TAB = [("tb%d" % k, 16) for k in range(4)]
     if rank is None:
-        TAB = [("taba", 4 * len(table_engines(topo, cores[own], core)))]
-    vset = [k for k in range(ns) if k % 4 == 3]
-    gth = {}
+        TAB = [("taba", sum(len(table_engines(topo, cores, mate, core, k)) for k in range(4)))]
+    gth = [[] for k in range(ns)]
+
+    def gather(a, b, vec):
+        out, ind = T.gt[:, a:b], T.tabx[:].indirect(T.offs[:, a // 16:b // 16])
+        w = TAB + [w3, t_lc]
+        gth[a // 1024].append(vcp(out, ind, w=w) if vec else act(out, ind, ACT.Copy, w=w))
+    cut = 1024 * ns - (256 if rank is None else 512)
     for k in range(ns):
-        ind = T.tabx[:].indirect(T.offs[:, 64 * k:64 * k + 64])
-        if k in vset:
-            gth[k] = vcp(T.gt[:, 1024 * k:1024 * k + 1024], ind, w=TAB + [w3, t_lc])
-        else:
-            gth[k] = act(T.gt[:, 1024 * k:1024 * k + 1024], ind, ACT.Copy, w=TAB + [w3, t_lc])
-    f1 = vtt(F("pm"), T.pq[:, 256:256 + n8], F("basew"), ALU.max, w=[m_q, b_w])
-    f2 = vtt(F("ne"), T.pq[:, 0:n8], F("pm"), ALU.is_gt, w=[f1])
-    f3 = vts(F("xx"), F("ne"), -65536.0, None, ALU.mult, w=[f2])
-    f4 = vtt(T.lf[:, 64:64 + n8], T.pq[:, 0:n8], F("ne"), ALU.mult)
-    f5 = vtt(F("x2"), F("xx"), F("trash"), ALU.add, w=[f3, g_tr])
-    f6 = vtt(T.lf[:, 0:n8], F("x2"), F("pm"), ALU.max, w=[f5])
-    f7 = vcp(T.lfu[:, 0:n8], T.lf[:, 0:n8], w=[f6])
-    f8 = vcp(T.lfu[:, 64:64 + n8], T.lf[:, 64:64 + n8], w=[f4])
-    fw = 16 + 1024 * ns + 1136
-    fl = vcp(T.flg[:, 0:fw].indirect(T.lfu[:, 0:n8]), T.lowt[:, 0:128 * nq], w=[f7, t_fl, t_lt])
+        gather(1024 * k, min(1024 * k + 1024, cut), False)
     if rank is not None:
-        z_q = vtt(C("zt"), T.zsb[:, 16:144], T.zsb[:, 15:143], ALU.is_equal, w=[s_z])
-        z_z = vts(C("zz"), C("zt"), -1.0, -LOW, ALU.add, ALU.mult, w=[z_q])
-    scn = []
-    for k in range(ns):
-        ini = LOW if k == 0 else T.sc[:, 15 + 1024 * k:16 + 1024 * k]
-        need("v", gth[k], fl, scn[k - 1] if k else t_gc)
-        scn.append(do("v", V.tensor_tensor_scan, T.sc[:, 16 + 1024 * k:1040 + 1024 * k], T.flg[:, 15 + 1024 * k:1039 + 1024 * k],
-                      T.gt[:, 1024 * k:1024 * k + 1024], ini, ALU.min, ALU.max))
-    done = {}
+        gather(cut, 1024 * ns, True)
+    h1 = vcp(T.hsm[:, :, 0:n8], T.pq[:, :, 0:n8], w=[m_q])
+    f0 = vtt(F("x2"), T.pq[:, 1, n8:2 * n8], T.hsm[:, 1, 0:n8], ALU.add, w=[h1])
+    f9 = vtt(F("qq"), T.pq[:, 0, n8:2 * n8], T.hsm[:, 0, 0:n8], ALU.add)
+    f1 = vtt(F("pm"), F("x2"), F("basew"), ALU.max, w=[f0, b_w])
+    f2 = vtt(F("ee"), F("qq"), F("pm"), ALU.is_le, w=[f1, f9])
+    f3 = vtt(F("xx"), F("ee"), F("trash"), ALU.mult, w=[f2, g_tr])
+    f6 = vtt(T.lf[:, 0:n8], F("xx"), F("pm"), ALU.max, w=[f3])
+    f7 = vcp(T.lfu[:, 0:n8], T.lf[:, 0:n8], w=[f6])
+    f4 = vtt(F("x2"), F("ee"), F("qq"), ALU.mult)
+    fw = 16 + 1024 * ns + 1136
+    fl = vcp(T.flg[:, 0:fw].indirect(T.lfu[:, 0:n8]), T.lowt[:, 0:128 * nq], w=[f7, t_fl, t_lt, t_fs])
+    f5 = vtt(T.lf[:, 64:64 + n8], F("qq"), F("x2"), ALU.subtract, w=[f4])
+    f8 = vcp(T.lfu[:, 64:64 + n8], T.lf[:, 64:64 + n8], w=[f5])
+    if rank is None:
+        gather(cut, 1024 * ns, True)
+    scn, done = [], {}
     gl = groups(part)
-    for gi, grp in enumerate(gl):
+
+    def pick(q, vec):
+        k = ready(part, q)
+        win = T.sc[:, 0:1040 + 1024 * k].indirect(T.lfu[:, 64 + 8 * (q - qlo):72 + 8 * (q - qlo)])
+        if vec:
+            done[q] = vcp(T.part[:, q - qlo, :], win, w=[scn[k], f8])
+        else:
+            done[q] = act(T.part[:, q - qlo, :], win, ACT.Copy, w=[scn[k], f8])
+
+    def send(grp):
         es = engines(topo, cores, part, grp)
-        order = [q for q in grp if q in es] + [q for q in grp if q not in es]
-        for n, q in enumerate(order):
-            qi = q - qlo
-            k = ready(part, q)
-            win = T.sc[:, 0:1040 + 1024 * k].indirect(T.lfu[:, 64 + 8 * qi:72 + 8 * qi])
-            if gi == len(gl) - 1 and n % 2 == 0:
-                done[q] = vcp(T.part[:, qi, :], win, w=[scn[k], f8])
-            else:
-                done[q] = act(T.part[:, qi, :], win, ACT.Copy, w=[scn[k], f8])
         tr = []
         for q in grp:
             if q in es:
@@ -385,6 +407,19 @@ def rank_program(g, core, T, topo):
             need("g", *[done[q] for q in es])
             g.remote_dma_fused(tr, local_sem=T.sem.loc)
             cnt["loc"] += sum(len(es[q]) for q in es)
+    for k in range(ns):
+        ini = LOW if k == 0 else T.sc[:, 15 + 1024 * k:16 + 1024 * k]
+        need("v", fl, scn[k - 1] if k else t_gc, *gth[k])
+        scn.append(do("v", V.tensor_tensor_scan, T.sc[:, 16 + 1024 * k:1040 + 1024 * k], T.flg[:, 15 + 1024 * k:1039 + 1024 * k],
+                      T.gt[:, 1024 * k:1024 * k + 1024], ini, ALU.min, ALU.max))
+        if len(gl) == 2 and k == max(ready(part, q) for q in gl[0]):
+            for q in gl[0]:
+                pick(q, False)
+            send(gl[0])
+    es = engines(topo, cores, part, gl[-1])
+    for n, q in enumerate([q for q in gl[-1] if q in es] + [q for q in gl[-1] if q not in es]):
+        pick(q, n % 2 == 0)
+    send(gl[-1])
     if rank is not None:
         arr = []
         for i, p in enumerate([p for p in parts if rank in p[4]]):
@@ -394,12 +429,16 @@ def rank_program(g, core, T, topo):
             else:
                 arr.append((gi, i, T.pland[:, i, :], ("pa%d" % i, len(engines(topo, cores, p, groups(p)[gi])[rank]))))
         arr.sort(key=lambda x: x[0:2])
-        acc, tok = C("zz"), z_z
-        for i, (_, _, ap, w) in enumerate(arr):
-            out = T.ysb[:] if i == len(arr) - 1 else T.pd[:, 0:128]
-            tok = vtt(out, acc, ap, ALU.max, w=[tok, w, m_d])
-            acc = out
-        need("y", tok)
+        ch = [[(T.pland[:, 16, :], ("zl", len(pool(topo, cores, mate))))] + [(x[2], x[3]) for x in arr[0::2]],
+              [(x[2], x[3]) for x in arr[1::2]]]
+        acc, tok = [ch[0][0][0], ch[1][0][0]], [ch[0][0][1], ch[1][0][1]]
+        for i in range(1, max(len(ch[0]), len(ch[1]))):
+            for j in range(2):
+                if i < len(ch[j]):
+                    out = C("zt") if j == 1 and i == len(ch[1]) - 1 else (T.pp, T.pa)[j][:, 0:128]
+                    tok[j] = vtt(out, acc[j], ch[j][i][0], ALU.max, w=[tok[j], ch[j][i][1]])
+                    acc[j] = out
+        need("y", vtt(T.ysb[:], acc[0], acc[1], ALU.max, w=tok))
         g.sync.dma_start(T.y[:], T.ysb[:]).then_inc(T.sem.yd, 16)
         need("y", ("yd", 16))
     need("g", *[(k, cnt[k]) for k in cnt])

@@ -1,11 +1,19 @@
 from concourse.bass import DstId, RemoteDMATransfer
 from concourse.mybir import AluOpType as ALU, ActivationFunctionType as ACT
 NR = 8
-HS = 4
 VB = [k for k in range(32) if k % 4 == 1]
 LAG = 4
-NB = 3
-LAY = (0, 1, 1, 0)
+KA = 3
+SRC = [(0, 2), (2, 4), (4, 6), (6, 8)]
+CHUNK = [1536, 1536, 1536, 1536, 1024, 512, 512]
+WAY = [{0: [1], 1: [2], 2: [3]}, {0: [1], 1: [3], 3: [2]}, {0: [1], 1: [2], 2: [3]}, {0: [1], 1: [3], 3: [2]},
+       {0: [1], 1: [2], 2: [3]}, {0: [1], 1: [2, 3]}, {0: [1], 1: [2, 3]}]
+ENG = "ahahaaa"
+NB = (4, 6)
+OFF = [sum(CHUNK[:k]) for k in range(len(CHUNK))]
+VECN = [384, 896, 896, 896]
+ZMAKER = 1
+MAKER = 3
 LOW = -201.0 * 2.0 ** 92
 NCORES = 128
 KC = ["i16", "cdv", "iota_a", "dwr", "dlt", "e0", "e1", "tri", "rep", "cd1", "cd2", "k1", "selx", "zt", "zz"]
@@ -13,8 +21,8 @@ KF = ["basew", "trash", "pm", "ee", "xx", "qq", "x2"]
 SPEC = {
     "float32": "cst 8,kf 7 64,hsm 2 64,pc 272,zsb 144,pay 4 32,msg 8 12,land 10 12,qm 4 8,lf 128",
     "bfloat16": "kc 15 128,tabx 8208,iota_b 64,zo 2 256,zs 136,osel 8,selw 8 128,selp 8 128,gge 256,sx 272,msk 384,col 4 32,"
-                "oa 32 128,ob1 32 64,ob2 32 64,lhl 2 64,qhl 2 8,flg 9344,lowt 1024,gt 8192,sc 8208,part 8 128,"
-                "pland 17 128,ysb 128",
+                "oa 32 128,ob1 32 64,ob2 32 64,lhl 2 64,qhl 2 8,flg 5248,lowt 1024,gt 4096,sc 4112,part 4 128,"
+                "pland 13 128,red 2 128,ysb 128",
     "int32": "idxa 256,idxe 32,pidx 4,pv 32,ti 32,e8 8", "float16": "gd 256,mg 384", "uint16": "cof 32,offs 512,lfu 128"}
 SCRATCH = {"ehd": ("dram", [128, 8], "int32")}
 for _dt in SPEC:
@@ -28,8 +36,8 @@ for _n, _sh, _dt in (("endw", [16, 64], "int32"), ("onef", [16, 128], "float32")
 for _n in ("pd", "pp", "pa", "pr", "px", "pn", "po"):
     SCRATCH[_n] = ("psum", [128, 512], "float32")
 SCRATCH["pq"] = ("psum", [128, 2, 256], "float32")
-SEMAPHORES = ["v", "s", "p", "gi", "ia", "ie", "en", "e8d", "eh", "zl", "tb0", "tb1", "tb2", "tb3", "yd", "arl", "loc", "taba"] \
-    + ["pa%d" % i for i in range(16)]
+SEMAPHORES = ["v", "s", "p", "gi", "ia", "ie", "en", "e8d", "eh", "zl", "yd", "arl", "arc", "sl", "loc"] \
+    + ["tb%d" % i for i in range(len(CHUNK))] + ["ra%d" % i for i in range(8)] + ["fa%d" % i for i in range(4)]
 
 
 def bits(m):
@@ -40,64 +48,79 @@ def emask(es):
     return sum(1 << e for e in es)
 
 
-def pool(topo, cores, c):
+def common(topo, core, dsts):
     es = list(range(16))
-    for d in cores:
-        if d != c:
-            es = [e for e in es if e in bits(topo.mask(c, d))]
+    for d in dsts:
+        if d != core:
+            es = [e for e in es if e in bits(topo.mask(core, d))]
     return es
 
 
-def table_engines(topo, cores, a, b, k):
-    es = pool(topo, cores, a)
-    return [e for e in bits(topo.mask(a, b)) if e not in es] if LAY[k] else es
-
-
-def plan(T, topo):
-    cores = list(T.cores)
-    parts = [(cores[o], o, 0, HS) for o in range(NR)]
-    used = []
-    for o in range(NR):
-        h = [c for c in range(NCORES) if topo.chip(c) == topo.chip(cores[o]) and c not in cores and c not in used
-             and all(topo.may_write(c, d) for d in cores)][0]
-        used.append(h)
-        parts.append((h, o, HS, NR))
-    return [p + ([q for q in range(NR) if q + 1 >= p[2] and q - 1 < p[3]],) for p in parts]
-
-
-def ready(part, q):
-    return min(q + 1, part[3] - 1) - part[2]
-
-
-def groups(part):
-    lim = part[3] - part[2] - (1 if part[2] == 0 else 2)
-    a = [q for q in part[4] if ready(part, q) < lim]
-    b = [q for q in part[4] if ready(part, q) >= lim]
-    return [x for x in (a, b) if x]
-
-
-def engines(topo, cores, part, grp):
-    dst = [q for q in grp if cores[q] != part[0]]
-    if not dst:
-        return {}
-    es = pool(topo, cores, part[0])
+def share(topo, core, dsts):
+    es = common(topo, core, dsts)
     n = 1
-    while 2 * n * len(dst) <= len(es):
+    while 2 * n * len(dsts) <= len(es) and n < 16:
         n *= 2
-    return {q: es[n * i:n * i + n] for i, q in enumerate(dst)}
+    return [es[n * i:n * i + n] for i in range(len(dsts))]
+
+
+def teams(T, topo):
+    cores = list(T.cores)
+    used = list(cores)
+    team = [[c, None, None, None] for c in cores]
+
+    def take(o, r, ok):
+        c = [c for c in range(NCORES) if topo.chip(c) == topo.chip(cores[o]) and c not in used and ok(c)][0]
+        used.append(c)
+        team[o][r] = c
+    for o in range(NR):
+        take(o, 2, lambda c: all(topo.may_write(c, d) for d in cores))
+    for o in range(NR):
+        take(o, 1, lambda c: topo.die(c) == topo.die(cores[o]))
+    for o in range(NR):
+        take(o, 3, lambda c: True)
+    return team
+
+
+def blocks(r):
+    return [q for q in range(NR) if q + 1 >= SRC[r][0] and q - 1 < SRC[r][1]]
+
+
+def ready(r, q):
+    return min(q + 1, SRC[r][1] - 1) - SRC[r][0]
+
+
+def early(r, q):
+    return ready(r, q) < SRC[r][1] - SRC[r][0] - 1
+
+
+def reducer(pair, q):
+    return pair[q % 2][0 if q < NR // 2 else 2]
+
+
+def inputs(pair, q):
+    a = [(t[r], r) for r in range(len(SRC)) for t in pair if q in blocks(r)]
+    return [x for x in a if early(x[1], q)] + [x for x in a if not early(x[1], q)]
+
+
+def outgoing(pair, c, r, e):
+    return [q for q in blocks(r) if early(r, q) == e and reducer(pair, q) != c]
 
 
 def rank_program(g, core, T, topo):
     cores = list(T.cores)
-    parts = plan(T, topo)
+    team = teams(T, topo)
     rank = T.rank_of(core)
-    mine = [p for p in parts if p[0] == core]
-    if not mine:
+    here = [(o, r) for o in range(NR) for r in range(len(SRC)) if team[o][r] == core]
+    if not here:
         return
-    part = mine[0]
-    own, s0, s1, blocks = part[1], part[2], part[3], part[4]
-    ns, nq, qlo = s1 - s0, len(blocks), blocks[0]
+    own, role = here[0]
+    s0, s1 = SRC[role]
+    blk = blocks(role)
+    ns, nq, qlo = s1 - s0, len(blk), blk[0]
     n8 = 8 * nq
+    chips = sorted(set(topo.chip(c) for c in cores))
+    pair = [t for t in team if topo.chip(t[0]) == topo.chip(core)]
     Q = {"v": g.vector, "s": g.scalar, "p": g.tensor, "g": g, "y": g.sync}
     SEM = {"v": "v", "s": "s", "p": "p", "g": "gi"}
     cnt = {"v": 0, "s": 0, "p": 0, "gi": 0, "loc": 0}
@@ -152,14 +175,15 @@ def rank_program(g, core, T, topo):
             return do("g", g.iota, out, pat, base, cm, allow_small_or_imprecise_dtypes=True)
         return do("g", g.iota, out, pat, base, cm)
 
-    def rdma(c, out, in_, sem, es):
-        a = topo.addr(c)
-        g.remote_dma(out, in_, T.sem[sem], T.sem.loc, a[1], a[0], emask(es))
-        cnt["loc"] += len(es)
-
     def dst(c):
         a = topo.addr(c)
         return DstId(rid=a[0], pnc=a[1])
+
+    def send(trs):
+        g.remote_dma_fused([RemoteDMATransfer(srcs=[s], dsts=[x[1] for x in d], dst_ids=[dst(x[0]) for x in d],
+                                              dma_engine_mask=emask(e), remote_sem=T.sem[m]) for s, d, e, m in trs],
+                           local_sem=T.sem.loc)
+        cnt["loc"] += sum(len(t[2]) for t in trs)
 
     def C(n, p=128, a=0, b=128):
         return T.kc[0:p, KC.index(n), a:b]
@@ -167,9 +191,12 @@ def rank_program(g, core, T, topo):
     def F(n):
         return T.kf[:, KF.index(n), 0:n8]
 
-    mate = [p[0] for p in parts if p[1] == own and p[0] != core][0]
-    es8 = pool(topo, cores, core)
+    es8 = common(topo, core, cores)
     IA, IE, EN = ("ia", 128), ("ie", 16), ("en", 16)
+
+    def chunk(k):
+        return T.tabx[:, OFF[k]:OFF[k] + CHUNK[k]]
+    TAB = [("tb%d" % k, 16) for k in range(len(CHUNK))]
     if rank is not None:
         g.sync.dma_start(T.e8[:], T.end[:]).then_inc(T.sem.e8d, 16)
         g.scalar.dma_start(T.endw[:], T.end[:]).then_inc(T.sem.en, 16)
@@ -177,10 +204,10 @@ def rank_program(g, core, T, topo):
             g.sync.dma_start(T.idxa[16 * o:16 * o + 16, :], T.idx[:]).then_inc(T.sem.ia, 16)
             g.scalar.dma_start(T.idxa[64 + 16 * o:80 + 16 * o, :], T.idx[:]).then_inc(T.sem.ia, 16)
         g.sync.dma_start(T.idxe[:], T.idx[:]).then_inc(T.sem.ie, 16)
-        for k in range(4):
-            g.sync.dma_start(T.tabx[:, 2048 * k:2048 * k + 2048], T.tab[:, 2048 * k:2048 * k + 2048]).then_inc(T.sem["tb%d" % k], 16)
-    else:
-        need("y", ("eh", len(pool(topo, cores, mate))))
+        for k in range(len(CHUNK)):
+            g.sync.dma_start(chunk(k), T.tab[:, OFF[k]:OFF[k] + CHUNK[k]]).then_inc(T.sem["tb%d" % k], 16)
+    elif role == ZMAKER:
+        need("y", ("eh", len(es8)))
         g.sync.dma_start(T.endw[:], T.ehd[:]).then_inc(T.sem.en, 16)
     pidx, cst = T.pidx, T.cst
     g_pi = iota(pidx[:, 0:1], [[0, 1]], 0, 1, False)
@@ -191,22 +218,32 @@ def rank_program(g, core, T, topo):
         g_ia = iota(C("iota_a"), [[1, 128]], 0, 0)
         g_ib = iota(T.iota_b[:], [[-128, 64]], 0, 0)
         need("g", ("e8d", 16))
-        rdma(mate, T.ehd[:], T.e8[:], "eh", es8)
+        send([(T.e8[:], [(team[own][ZMAKER], T.ehd[:])], es8, "eh")])
     g_dw = iota(C("dwr"), [[0, 8], [-1, 16]], 0, 1)
     g_bm = iota(T.qm[:, 3, 0:nq], [[1024, nq]], 1024 * (qlo - 1 - s0), 0)
     g_bw = iota(F("basew"), [[1024, nq], [0, 8]], 1024 * (qlo - 1 - s0), 0)
     g_tr = iota(F("trash"), [[16, n8]], 16 + 1024 * ns, 1)
+
+    def table_engines(k, r):
+        es = common(topo, team[own][r], [team[own][x] for x in WAY[k][r]])
+        if r == 0 and ENG[k] == "h":
+            es = [e for e in es if e not in common(topo, team[own][r], cores)]
+        return es
+
+    def table_on(a, b):
+        for k in range(a, b):
+            if role in WAY[k]:
+                need("g", TAB[k])
+                send([(chunk(k), [(team[own][x], chunk(k)) for x in WAY[k][role]], table_engines(k, role), "tb%d" % k)])
+    if rank is None:
+        for k in range(len(CHUNK)):
+            TAB[k] = ("tb%d" % k, len(table_engines(k, [r for r in WAY[k] if role in WAY[k][r]][0])))
+    else:
+        table_on(0, NB[0])
     local, t_ld = False, None
     t_fs = None
-
-    def table_on(k):
-        need("g", ("tb%d" % k, 16))
-        rdma(mate, T.tabx[:, 2048 * k:2048 * k + 2048], T.tabx[:, 2048 * k:2048 * k + 2048], "taba",
-             table_engines(topo, cores, core, mate, k))
     ri = vts(pidx[:, 2:3], pidx[:, 0:1], 15, None, ALU.bitwise_and, w=[g_pi])
     if rank is not None:
-        for k in range(NB):
-            table_on(k)
         hb = [q for q in (rank - 1, rank, rank + 1) if 0 <= q < NR]
         nc = 8 * len(hb)
         ca = 8 * hb[0]
@@ -262,6 +299,7 @@ def rank_program(g, core, T, topo):
         a1 = vts(T.ti[:], T.pa[:, 0:32], 1.0 / 128, -0.496, ALU.mult, ALU.add, w=[m_a])
         a2 = vts(tb, T.ti[:], -128.0, None, ALU.mult, w=[a1])
         a3 = vtt(mb, T.pa[:, 0:32], tb, ALU.add, w=[a2])
+        tg = [(team[o][r], o) for o in range(NR) for r in range(len(SRC)) if SRC[r][0] <= rank < SRC[r][1] and team[o][r] != core]
         lag = {}
 
         def low_mm(j, stop):
@@ -276,53 +314,60 @@ def rank_program(g, core, T, topo):
             mm(T.px[:, 0:64], T.oa[:, k, :], T.ob1[:, k, :], k == 0, False, w=[o_b])
             if k >= LAG:
                 low_mm(k - LAG, False)
-            if k == 5:
+            if k == KA:
                 t_co = vcp(T.cof[:, 0:nc], T.pn[:, 0:nc], w=[m_c])
                 t_p2 = vts(T.pc[:, 256:272], T.zo[:, 1, 0:16], cst[:, 4:5], None, ALU.mult)
                 t_os = vts(T.osel[:], T.kc[:, KC.index("cdv"), 0:128:16], cst[:, 0:1], 0.0, ALU.add, ALU.is_le)
                 t_ms = vms(T.msg[:], 0.0)
-            if k == 8:
+            if k == KA + 1:
                 t_mk = vts(T.msk[:, 0:16 * nc], T.pr[:, 0:16 * nc], cst[:, 1:2], None, ALU.is_equal, w=[m_r])
-            if k == 14:
+            if k == KA + 3:
                 t_mg = vtt(T.mg[:, 0:16 * nc], T.pc[:].indirect(T.cof[:, 0:nc]), T.msk[:, 0:16 * nc], ALU.mult,
                            w=[t_co, t_p2, s_pc, t_mk])
-            if k == 20:
+            if k == KA + 6:
                 for j in range(len(hb)):
                     m_n = mm(T.pn[:, 128 + 8 * j:136 + 8 * j], T.mg[:, 128 * j:128 * j + 128], T.osel[:], True, True, w=[t_mg, t_os, t_co])
+            if k == KA + 8:
+                for j, q in enumerate(hb):
+                    t_mc = vcp(T.msg[:, :, 8 + q - rank + 1], T.pn[:, 128 + 8 * j:136 + 8 * j], w=[m_n, t_ms])
+                need("g", t_mc)
+                send([(T.msg[:, o, 8:12], [(c, T.land[:, rank + 1, 8:12])], [e], "arc") for (c, o), e in zip(tg, es8)])
+                table_on(NB[0], NB[1])
         for j in range(32 - LAG, 32):
             m_x = low_mm(j, j == 31)
-        for j, q in enumerate(hb):
-            vcp(T.msg[:, :, 8 + q - rank + 1], T.pn[:, 128 + 8 * j:136 + 8 * j], w=[m_n, t_ms])
         t_mx = vcp(T.msg[:, :, 0:8], T.px[:, 0:64], w=[m_x])
-        tg = [p for p in parts if p[2] <= rank < p[3] and p[0] != core]
         need("g", t_mx)
-        g.remote_dma_fused([RemoteDMATransfer(src=T.msg[:, p[1], :], dst=T.land[:, rank + 1, :], dst_ids=[dst(p[0])],
-                                              dma_engine_mask=emask([e]), remote_sem=T.sem.arl) for p, e in zip(tg, es8)],
-                           local_sem=T.sem.loc)
-        cnt["loc"] += len(tg)
-        for k in range(NB, 4):
-            table_on(k)
+        send([(T.msg[:, o, 0:8], [(c, T.land[:, rank + 1, 0:8])], [e], "arl") for (c, o), e in zip(tg, es8)])
+        table_on(NB[1], len(CHUNK))
         local = s0 <= rank < s1
         if local:
-            t_ld = vcp(T.land[:, rank + 1, :], T.msg[:, own, :], w=[t_mx])
-        t_fs = act(T.flg[:, 16 + 512 * ns:16 + 1024 * ns], T.oa[:, 0:4 * ns, :], ACT.Identity, w=[t_mx], bias=-LOW, scale=0.0)
+            t_ld = vcp(T.land[:, rank + 1, :], T.msg[:, own, :], w=[t_mx, t_mc])
+        t_fs = act(T.flg[:, 16:16 + 1024 * ns], T.oa[:, 0:8 * ns, :], ACT.Identity, w=[t_mx], bias=-LOW, scale=0.0)
     else:
         c_rf = vcp(cst[:, 1:2], pidx[:, 2:3], w=[ri])
         t_id = vts(T.id16[:], C("i16", 16, 0, 16), cst[0:16, 1:2], None, ALU.is_equal, w=[c_rf, g_16])
-    for k in range(8):
-        t_sw = vts(T.selw[:, k, :], C("dwr"), 16.0 * k, None, ALU.is_equal, w=[g_dw])
+    sel_es = share(topo, team[own][MAKER], [team[own][0]] * 2)
+    if rank is not None:
+        t_sw = t_sp = ("sl", len(sel_es[0]) + len(sel_es[1]))
+    else:
+        for k in range(8):
+            t_sw = vts(T.selw[:, k, :], C("dwr"), 16.0 * k, None, ALU.is_equal, w=[g_dw])
+        for k in range(8):
+            t_sp = vts(T.selp[:, k, :], C("dwr"), 16.0 * k - 1.0, None, ALU.is_equal)
+        if role == MAKER:
+            need("g", t_sw, t_sp)
+            send([(x, [(team[own][0], x)], e, "sl") for x, e in zip((T.selw[:], T.selp[:]), sel_es)])
+        table_on(0, len(CHUNK))
     z0 = vms(T.land[:, 0:s0 + 1, :], 0.0)
     z1 = vms(T.land[:, s1 + 1:10, :], 0.0)
     b_m = vts(T.qm[:, 3, 0:nq], T.qm[:, 3, 0:nq], 0.0, 15.0, ALU.max, ALU.add, w=[g_bm])
     b_w = vts(F("basew"), F("basew"), 0.0, 15.0, ALU.max, ALU.add, w=[g_bw])
-    for k in range(8):
-        t_sp = vts(T.selp[:, k, :], C("dwr"), 16.0 * k - 1.0, None, ALU.is_equal)
-    t_sp = vts(C("selx"), C("dwr"), 127.0, None, ALU.is_equal)
+    t_sx = vts(C("selx"), C("dwr"), 127.0, None, ALU.is_equal, w=[g_dw])
     t_lc = vms(T.tabx[:, 8192:8208], LOW)
     t_gc = vms(T.sc[:, 0:16], LOW)
     t_lt = vms(T.lowt[:, 0:128 * nq], LOW)
-    t_fl = vms(T.flg[:, 0:16 + (1024 if t_fs is None else 512) * ns], -LOW)
-    if rank is None:
+    t_fl = vms(T.flg[:, 0:16 + (1024 * ns if t_fs is None else 0)], -LOW)
+    if role == ZMAKER:
         za = 0 if own > 0 else 1
         t_of = vms(T.onef[:], 1.0)
         z_m = vms(T.zsb[:, 0:16], 0.0)
@@ -334,41 +379,21 @@ def rank_program(g, core, T, topo):
         z_q = vtt(C("zt"), T.zsb[:, 16:144], T.zsb[:, 15:143], ALU.is_equal, w=[s_z, z_m])
         z_z = vts(C("zz"), C("zt"), -1.0, -LOW, ALU.add, ALU.mult, w=[z_q])
         need("g", z_z)
-        rdma(mate, T.pland[:, 16, :], C("zz"), "zl", es8)
-    AR = ("arl", ns - (1 if local else 0))
+        send([(C("zz"), [(team[own][0], T.pland[:, 12, :])], share(topo, core, [team[own][0]])[0], "zl")])
+    far = ns - (1 if local else 0)
     L = T.land
-    lhi, llo, qhi, qlw = T.lhl[:, 0, 0:8 * ns], T.lhl[:, 1, 0:8 * ns], T.qhl[:, 0, 0:nq], T.qhl[:, 1, 0:nq]
-    w1 = vcp(lhi, L[:, s0 + 1:s1 + 1, 0:8], w=[AR, t_ld])
-    w2 = vtt(llo, L[:, s0 + 1:s1 + 1, 0:8], lhi, ALU.subtract, w=[w1])
-    for k in range(8):
-        mm(T.po[:, k:64 * ns:8], T.selw[:, k, :], lhi, True, False, w=[w1, t_sw])
-        m_o = mm(T.po[:, k:64 * ns:8], T.selw[:, k, :], llo, False, True, w=[w2])
-    q1 = vtt(T.qm[:, 0, 0:nq], L[:, qlo:qlo + nq, 10], L[:, qlo + 1:qlo + 1 + nq, 9], ALU.add, w=[z0, z1])
+    qhi, qlw = T.qhl[:, 0, 0:nq], T.qhl[:, 1, 0:nq]
+    q1 = vtt(T.qm[:, 0, 0:nq], L[:, qlo:qlo + nq, 10], L[:, qlo + 1:qlo + 1 + nq, 9], ALU.add, w=[z0, z1, t_ld, ("arc", far)])
     q2 = vtt(T.qm[:, 1, 0:nq], T.qm[:, 0, 0:nq], L[:, qlo + 2:qlo + 2 + nq, 8], ALU.add, w=[q1])
     q3 = vtt(T.qm[:, 2, 0:nq], T.qm[:, 1, 0:nq], T.qm[:, 3, 0:nq], ALU.add, w=[q2, b_m])
     q4 = vcp(qhi, T.qm[:, 2, 0:nq], w=[q3])
     q5 = vtt(qlw, T.qm[:, 2, 0:nq], qhi, ALU.subtract, w=[q4])
-    w3 = vts(T.offs[:, 0:64 * ns], T.po[:, 0:64 * ns], -1.0, 8192.0, ALU.mult, ALU.add, w=[m_o])
     for k in range(8):
-        mm(T.pq[:, 0, k:2 * n8:8], T.selw[:, k, :], T.qhl[:, :, 0:nq], True, True, w=[q4, q5])
+        mm(T.pq[:, 0, k:2 * n8:8], T.selw[:, k, :], T.qhl[:, :, 0:nq], True, True, w=[q4, q5, t_sw])
         m_q = mm(T.pq[:, 1, k:2 * n8:8], T.selp[:, k, :], T.qhl[:, :, 0:nq], True, k > 0, w=[t_sp])
         if k == 0:
-            mm(T.pq[:, 1, 8:n8:8], C("selx"), T.qhl[:, 0, 0:nq - 1], False, False)
+            mm(T.pq[:, 1, 8:n8:8], C("selx"), T.qhl[:, 0, 0:nq - 1], False, False, w=[t_sx])
             mm(T.pq[:, 1, n8 + 8:2 * n8:8], C("selx"), T.qhl[:, 1, 0:nq - 1], False, True)
-    TAB = [("tb%d" % k, 16) for k in range(4)]
-    if rank is None:
-        TAB = [("taba", sum(len(table_engines(topo, cores, mate, core, k)) for k in range(4)))]
-    gth = [[] for k in range(ns)]
-
-    def gather(a, b, vec):
-        out, ind = T.gt[:, a:b], T.tabx[:].indirect(T.offs[:, a // 16:b // 16])
-        w = TAB + [w3, t_lc]
-        gth[a // 1024].append(vcp(out, ind, w=w) if vec else act(out, ind, ACT.Copy, w=w))
-    cut = 1024 * ns - (256 if rank is None else 512)
-    for k in range(ns):
-        gather(1024 * k, min(1024 * k + 1024, cut), False)
-    if rank is not None:
-        gather(cut, 1024 * ns, True)
     h1 = vcp(T.hsm[:, :, 0:n8], T.pq[:, :, 0:n8], w=[m_q])
     f0 = vtt(F("x2"), T.pq[:, 1, n8:2 * n8], T.hsm[:, 1, 0:n8], ALU.add, w=[h1])
     f9 = vtt(F("qq"), T.pq[:, 0, n8:2 * n8], T.hsm[:, 0, 0:n8], ALU.add)
@@ -379,66 +404,102 @@ def rank_program(g, core, T, topo):
     f7 = vcp(T.lfu[:, 0:n8], T.lf[:, 0:n8], w=[f6])
     f4 = vtt(F("x2"), F("ee"), F("qq"), ALU.mult)
     fw = 16 + 1024 * ns + 1136
-    fl = vcp(T.flg[:, 0:fw].indirect(T.lfu[:, 0:n8]), T.lowt[:, 0:128 * nq], w=[f7, t_fl, t_lt, t_fs])
     f5 = vtt(T.lf[:, 64:64 + n8], F("qq"), F("x2"), ALU.subtract, w=[f4])
     f8 = vcp(T.lfu[:, 64:64 + n8], T.lf[:, 64:64 + n8], w=[f5])
+
+    def flags():
+        return vcp(T.flg[:, 0:fw].indirect(T.lfu[:, 0:n8]), T.lowt[:, 0:128 * nq], w=[f7, t_fl, t_lt, t_fs])
     if rank is None:
+        fl = flags()
+    lhi, llo = T.lhl[:, 0, 0:8 * ns], T.lhl[:, 1, 0:8 * ns]
+    w1 = vcp(lhi, L[:, s0 + 1:s1 + 1, 0:8], w=[("arl", far), t_ld])
+    w2 = vtt(llo, L[:, s0 + 1:s1 + 1, 0:8], lhi, ALU.subtract, w=[w1])
+    for k in range(8):
+        mm(T.po[:, k:64 * ns:8], T.selw[:, k, :], lhi, True, False, w=[w1, t_sw])
+        m_o = mm(T.po[:, k:64 * ns:8], T.selw[:, k, :], llo, False, True, w=[w2])
+    w3 = vts(T.offs[:, 0:64 * ns], T.po[:, 0:64 * ns], -1.0, 8192.0, ALU.mult, ALU.add, w=[m_o])
+    gth = [[] for k in range(ns)]
+
+    def gather(a, b, vec):
+        out, ind = T.gt[:, a:b], T.tabx[:].indirect(T.offs[:, a // 16:b // 16])
+        w = TAB + [w3, t_lc]
+        gth[a // 1024].append(vcp(out, ind, w=w) if vec else act(out, ind, ACT.Copy, w=w))
+    cut = 1024 * ns - VECN[role]
+    for k in range(ns):
+        if 1024 * k < cut:
+            gather(1024 * k, min(1024 * k + 1024, cut), False)
+    if rank is not None:
+        fl = flags()
+    if cut < 1024 * ns:
         gather(cut, 1024 * ns, True)
     scn, done = [], {}
-    gl = groups(part)
 
     def pick(q, vec):
-        k = ready(part, q)
+        k = ready(role, q)
         win = T.sc[:, 0:1040 + 1024 * k].indirect(T.lfu[:, 64 + 8 * (q - qlo):72 + 8 * (q - qlo)])
         if vec:
             done[q] = vcp(T.part[:, q - qlo, :], win, w=[scn[k], f8])
         else:
             done[q] = act(T.part[:, q - qlo, :], win, ACT.Copy, w=[scn[k], f8])
 
-    def send(grp):
-        es = engines(topo, cores, part, grp)
-        tr = []
-        for q in grp:
-            if q in es:
-                sl = [p[0] for p in parts if q in p[4]].index(core)
-                tr.append(RemoteDMATransfer(src=T.part[:, q - qlo, :], dst=T.pland[:, sl, :], dst_ids=[dst(cores[q])],
-                                            dma_engine_mask=emask(es[q]), remote_sem=T.sem["pa%d" % sl]))
-        if tr:
-            need("g", *[done[q] for q in es])
-            g.remote_dma_fused(tr, local_sem=T.sem.loc)
-            cnt["loc"] += sum(len(es[q]) for q in es)
+    def pass_on(qs):
+        if qs:
+            red = [reducer(pair, q) for q in qs]
+            idx = [4 * (q % 4 // 2) + inputs(pair, q).index((core, role)) for q in qs]
+            need("g", *[done[q] for q in qs])
+            send([(T.part[:, q - qlo, :], [(c, T.pland[:, i, :])], e, "ra%d" % i)
+                  for q, c, e, i in zip(qs, red, share(topo, core, red), idx)])
+    soon = [q for q in blk if early(role, q)]
     for k in range(ns):
         ini = LOW if k == 0 else T.sc[:, 15 + 1024 * k:16 + 1024 * k]
         need("v", fl, scn[k - 1] if k else t_gc, *gth[k])
         scn.append(do("v", V.tensor_tensor_scan, T.sc[:, 16 + 1024 * k:1040 + 1024 * k], T.flg[:, 15 + 1024 * k:1039 + 1024 * k],
                       T.gt[:, 1024 * k:1024 * k + 1024], ini, ALU.min, ALU.max))
-        if len(gl) == 2 and k == max(ready(part, q) for q in gl[0]):
-            for q in gl[0]:
+        if soon and k == max(ready(role, q) for q in soon):
+            for q in soon:
                 pick(q, False)
-            send(gl[0])
-    es = engines(topo, cores, part, gl[-1])
-    for n, q in enumerate([q for q in gl[-1] if q in es] + [q for q in gl[-1] if q not in es]):
+            pass_on(outgoing(pair, core, role, True))
+    out = outgoing(pair, core, role, False)
+    for n, q in enumerate(out + [q for q in blk if q not in out and q not in done]):
         pick(q, n % 2 == 0)
-    send(gl[-1])
-    if rank is not None:
-        arr = []
-        for i, p in enumerate([p for p in parts if rank in p[4]]):
-            gi = [j for j, x in enumerate(groups(p)) if rank in x][0]
-            if p[0] == core:
-                arr.append((gi, -1, T.part[:, rank - qlo, :], done[rank]))
+    pass_on(out)
+    t_red = {}
+    for q in range(NR):
+        if reducer(pair, q) != core:
+            continue
+        qi = q % 4 // 2
+        ins = []
+        for i, (c, r) in enumerate(inputs(pair, q)):
+            if c == core:
+                ins.append((T.part[:, q - qlo, :], done[q]))
             else:
-                arr.append((gi, i, T.pland[:, i, :], ("pa%d" % i, len(engines(topo, cores, p, groups(p)[gi])[rank]))))
-        arr.sort(key=lambda x: x[0:2])
-        ch = [[(T.pland[:, 16, :], ("zl", len(pool(topo, cores, mate))))] + [(x[2], x[3]) for x in arr[0::2]],
-              [(x[2], x[3]) for x in arr[1::2]]]
-        acc, tok = [ch[0][0][0], ch[1][0][0]], [ch[0][0][1], ch[1][0][1]]
-        for i in range(1, max(len(ch[0]), len(ch[1]))):
-            for j in range(2):
-                if i < len(ch[j]):
-                    out = C("zt") if j == 1 and i == len(ch[1]) - 1 else (T.pp, T.pa)[j][:, 0:128]
-                    tok[j] = vtt(out, acc[j], ch[j][i][0], ALU.max, w=[tok[j], ch[j][i][1]])
-                    acc[j] = out
-        need("y", vtt(T.ysb[:], acc[0], acc[1], ALU.max, w=tok))
+                o = outgoing(pair, c, r, early(r, q))
+                ins.append((T.pland[:, 4 * qi + i, :], ("ra%d" % (4 * qi + i), len(share(topo, c, [reducer(pair, x) for x in o])[0]))))
+        acc, tok = ins[0]
+        for i in range(1, len(ins)):
+            res = T.red[:, qi, :] if i == len(ins) - 1 else (T.pp, T.pa)[qi][:, 0:128]
+            tok = vtt(res, acc, ins[i][0], ALU.max, w=[tok, ins[i][1]])
+            acc = res
+        t_red[q] = tok
+        if cores[q] != core:
+            ci = chips.index(topo.chip(core))
+            need("g", tok)
+            send([(T.red[:, qi, :], [(cores[q], T.pland[:, 8 + ci, :])], share(topo, core, [cores[q]])[0], "fa%d" % ci)])
+    if rank is not None:
+        near, away = [(T.pland[:, 12, :], ("zl", len(share(topo, team[own][ZMAKER], [core])[0])))], []
+        for ci, ch in enumerate(chips):
+            c = reducer([t for t in team if topo.chip(t[0]) == ch], rank)
+            if c == core:
+                near.append((T.red[:, rank % 4 // 2, :], t_red[rank]))
+            else:
+                (near if ch == topo.chip(core) else away).append((T.pland[:, 8 + ci, :], ("fa%d" % ci, len(share(topo, c, [core])[0]))))
+        ins = near + away
+        acc, tok = ins[0]
+        for i in range(1, len(ins)):
+            res = T.ysb[:] if i == len(ins) - 1 else T.pd[:, 0:128]
+            tok = vtt(res, acc, ins[i][0], ALU.max, w=[tok, ins[i][1]])
+            acc = res
+        need("y", tok)
         g.sync.dma_start(T.y[:], T.ysb[:]).then_inc(T.sem.yd, 16)
         need("y", ("yd", 16))
     need("g", *[(k, cnt[k]) for k in cnt])

from concourse.bass import DstId, RemoteDMATransfer
from concourse.mybir import AluOpType as ALU, ActivationFunctionType as ACT
NR = 8
VB = [k for k in range(32) if k % 4 == 1]
LAG = 4
KA = 3
SRC = [(0, 2), (2, 4), (4, 6), (6, 8)]
CHUNK = [1536, 1536, 1536, 1536, 1024, 512, 512]
WAY = [{0: [1], 1: [2], 2: [3]}, {0: [1], 1: [3], 3: [2]}, {0: [1], 1: [2], 2: [3]}, {0: [1], 1: [3], 3: [2]},
       {0: [1], 1: [2], 2: [3]}, {0: [1], 1: [2, 3]}, {0: [1], 1: [2, 3]}]
ENG = "ahahaaa"
NB = (4, 6)
OFF = [sum(CHUNK[:k]) for k in range(len(CHUNK))]
VECN = [384, 896, 896, 896]
ZMAKER = 1
MAKER = 3
LOW = -201.0 * 2.0 ** 92
NCORES = 128
KC = ["i16", "cdv", "iota_a", "dwr", "dlt", "e0", "e1", "tri", "rep", "cd1", "cd2", "k1", "selx", "zt", "zz"]
KF = ["basew", "trash", "pm", "ee", "xx", "qq", "x2"]
SPEC = {
    "float32": "cst 8,kf 7 64,hsm 2 64,pc 272,zsb 144,pay 4 32,msg 8 12,land 10 12,qm 4 8,lf 128",
    "bfloat16": "kc 15 128,tabx 8208,iota_b 64,zo 2 256,zs 136,osel 8,selw 8 128,selp 8 128,gge 256,sx 272,msk 384,col 4 32,"
                "oa 32 128,ob1 32 64,ob2 32 64,lhl 2 64,qhl 2 8,flg 5248,lowt 1024,gt 4096,sc 4112,part 4 128,"
                "pland 13 128,red 2 128,ysb 128",
    "int32": "idxa 256,idxe 32,pidx 4,pv 32,ti 32,e8 8", "float16": "gd 256,mg 384", "uint16": "cof 32,offs 512,lfu 128"}
SCRATCH = {"ehd": ("dram", [128, 8], "int32")}
for _dt in SPEC:
    for _e in SPEC[_dt].split(","):
        _w = _e.split()
        SCRATCH[_w[0]] = ("sbuf", [128] + [int(x) for x in _w[1:]], _dt)
for _n, _sh, _dt in (("endw", [16, 64], "int32"), ("onef", [16, 128], "float32"), ("id16", [16, 16], "float32"),
                     ("ei", [16, 4, 32], "int32"), ("cbf", [16, 24], "bfloat16"), ("rbf", [16, 24], "bfloat16"),
                     ("rdg", [16, 24, 16], "bfloat16"), ("ef", [16, 9], "float32"), ("zdg", [16, 9, 16], "float32")):
    SCRATCH[_n] = ("sbuf", _sh, _dt)
for _n in ("pd", "pp", "pa", "pr", "px", "pn", "po"):
    SCRATCH[_n] = ("psum", [128, 512], "float32")
SCRATCH["pq"] = ("psum", [128, 2, 256], "float32")
SEMAPHORES = ["v", "s", "p", "gi", "ia", "ie", "en", "e8d", "eh", "zl", "yd", "arl", "arc", "sl", "loc"] \
    + ["tb%d" % i for i in range(len(CHUNK))] + ["ra%d" % i for i in range(8)] + ["fa%d" % i for i in range(4)]


def bits(m):
    return [i for i in range(16) if (m >> i) & 1]


def emask(es):
    return sum(1 << e for e in es)


def common(topo, core, dsts):
    es = list(range(16))
    for d in dsts:
        if d != core:
            es = [e for e in es if e in bits(topo.mask(core, d))]
    return es


def share(topo, core, dsts):
    es = common(topo, core, dsts)
    n = 1
    while 2 * n * len(dsts) <= len(es) and n < 16:
        n *= 2
    return [es[n * i:n * i + n] for i in range(len(dsts))]


def teams(T, topo):
    cores = list(T.cores)
    used = list(cores)
    team = [[c, None, None, None] for c in cores]

    def take(o, r, ok):
        c = [c for c in range(NCORES) if topo.chip(c) == topo.chip(cores[o]) and c not in used and ok(c)][0]
        used.append(c)
        team[o][r] = c
    for o in range(NR):
        take(o, 2, lambda c: all(topo.may_write(c, d) for d in cores))
    for o in range(NR):
        take(o, 1, lambda c: topo.die(c) == topo.die(cores[o]))
    for o in range(NR):
        take(o, 3, lambda c: True)
    return team


def blocks(r):
    return [q for q in range(NR) if q + 1 >= SRC[r][0] and q - 1 < SRC[r][1]]


def ready(r, q):
    return min(q + 1, SRC[r][1] - 1) - SRC[r][0]


def early(r, q):
    return ready(r, q) < SRC[r][1] - SRC[r][0] - 1


def reducer(pair, q):
    return pair[q % 2][0 if q < NR // 2 else 2]


def inputs(pair, q):
    a = [(t[r], r) for r in range(len(SRC)) for t in pair if q in blocks(r)]
    return [x for x in a if early(x[1], q)] + [x for x in a if not early(x[1], q)]


def outgoing(pair, c, r, e):
    return [q for q in blocks(r) if early(r, q) == e and reducer(pair, q) != c]


def rank_program(g, core, T, topo):
    cores = list(T.cores)
    team = teams(T, topo)
    rank = T.rank_of(core)
    here = [(o, r) for o in range(NR) for r in range(len(SRC)) if team[o][r] == core]
    if not here:
        return
    own, role = here[0]
    s0, s1 = SRC[role]
    blk = blocks(role)
    ns, nq, qlo = s1 - s0, len(blk), blk[0]
    n8 = 8 * nq
    chips = sorted(set(topo.chip(c) for c in cores))
    pair = [t for t in team if topo.chip(t[0]) == topo.chip(core)]
    Q = {"v": g.vector, "s": g.scalar, "p": g.tensor, "g": g, "y": g.sync}
    SEM = {"v": "v", "s": "s", "p": "p", "g": "gi"}
    cnt = {"v": 0, "s": 0, "p": 0, "gi": 0, "loc": 0}
    seen = {}

    def need(q, *toks):
        best = {}
        for t in toks:
            if t is not None:
                best[t[0]] = max(best.get(t[0], 0), t[1])
        for sem in best:
            if seen.get((q, sem), 0) < best[sem]:
                Q[q].wait_ge(T.sem[sem], best[sem])
                seen[(q, sem)] = best[sem]

    def do(q, call, *args, **kw):
        sem = SEM[q]
        call(*args, **kw).then_inc(T.sem[sem], 1)
        cnt[sem] += 1
        return (sem, cnt[sem])

    V, S, P = g.vector, g.scalar, g.tensor

    def vts(out, in0, a, b, op0, op1=None, w=()):
        need("v", *w)
        if op1 is None:
            return do("v", V.tensor_scalar, out, in0, a, b, op0)
        return do("v", V.tensor_scalar, out, in0, a, b, op0, op1)

    def vtt(out, a, b, op, w=()):
        need("v", *w)
        return do("v", V.tensor_tensor, out, a, b, op)

    def vcp(out, a, w=()):
        need("v", *w)
        return do("v", V.tensor_copy, out, a)

    def vms(ap, c, w=()):
        need("v", *w)
        return do("v", V.memset, ap, c)

    def act(out, in_, func, w=(), **kw):
        need("s", *w)
        return do("s", S.activation, out, in_, func, **kw)

    def mm(out, l, r, start, stop, w=()):
        need("p", *w)
        return do("p", P.matmul, out, l, r, start, stop)

    def iota(out, pat, base, cm, flag=True):
        if flag:
            return do("g", g.iota, out, pat, base, cm, allow_small_or_imprecise_dtypes=True)
        return do("g", g.iota, out, pat, base, cm)

    def dst(c):
        a = topo.addr(c)
        return DstId(rid=a[0], pnc=a[1])

    def send(trs):
        g.remote_dma_fused([RemoteDMATransfer(srcs=[s], dsts=[x[1] for x in d], dst_ids=[dst(x[0]) for x in d],
                                              dma_engine_mask=emask(e), remote_sem=T.sem[m]) for s, d, e, m in trs],
                           local_sem=T.sem.loc)
        cnt["loc"] += sum(len(t[2]) for t in trs)

    def C(n, p=128, a=0, b=128):
        return T.kc[0:p, KC.index(n), a:b]

    def F(n):
        return T.kf[:, KF.index(n), 0:n8]

    es8 = common(topo, core, cores)
    IA, IE, EN = ("ia", 128), ("ie", 16), ("en", 16)

    def chunk(k):
        return T.tabx[:, OFF[k]:OFF[k] + CHUNK[k]]
    TAB = [("tb%d" % k, 16) for k in range(len(CHUNK))]
    if rank is not None:
        g.sync.dma_start(T.e8[:], T.end[:]).then_inc(T.sem.e8d, 16)
        g.scalar.dma_start(T.endw[:], T.end[:]).then_inc(T.sem.en, 16)
        for o in range(4):
            g.sync.dma_start(T.idxa[16 * o:16 * o + 16, :], T.idx[:]).then_inc(T.sem.ia, 16)
            g.scalar.dma_start(T.idxa[64 + 16 * o:80 + 16 * o, :], T.idx[:]).then_inc(T.sem.ia, 16)
        g.sync.dma_start(T.idxe[:], T.idx[:]).then_inc(T.sem.ie, 16)
        for k in range(len(CHUNK)):
            g.sync.dma_start(chunk(k), T.tab[:, OFF[k]:OFF[k] + CHUNK[k]]).then_inc(T.sem["tb%d" % k], 16)
    elif role == ZMAKER:
        need("y", ("eh", len(es8)))
        g.sync.dma_start(T.endw[:], T.ehd[:]).then_inc(T.sem.en, 16)
    pidx, cst = T.pidx, T.cst
    g_pi = iota(pidx[:, 0:1], [[0, 1]], 0, 1, False)
    if rank is not None:
        g_cd = iota(C("cdv"), [[-1, 8], [0, 16]], 0, 0)
    g_16 = iota(C("i16"), [[0, 8], [1, 16]], 0, 0)
    if rank is not None:
        g_ia = iota(C("iota_a"), [[1, 128]], 0, 0)
        g_ib = iota(T.iota_b[:], [[-128, 64]], 0, 0)
        need("g", ("e8d", 16))
        send([(T.e8[:], [(team[own][ZMAKER], T.ehd[:])], es8, "eh")])
    g_dw = iota(C("dwr"), [[0, 8], [-1, 16]], 0, 1)
    g_bm = iota(T.qm[:, 3, 0:nq], [[1024, nq]], 1024 * (qlo - 1 - s0), 0)
    g_bw = iota(F("basew"), [[1024, nq], [0, 8]], 1024 * (qlo - 1 - s0), 0)
    g_tr = iota(F("trash"), [[16, n8]], 16 + 1024 * ns, 1)

    def table_engines(k, r):
        es = common(topo, team[own][r], [team[own][x] for x in WAY[k][r]])
        if r == 0 and ENG[k] == "h":
            es = [e for e in es if e not in common(topo, team[own][r], cores)]
        return es

    def table_on(a, b):
        for k in range(a, b):
            if role in WAY[k]:
                need("g", TAB[k])
                send([(chunk(k), [(team[own][x], chunk(k)) for x in WAY[k][role]], table_engines(k, role), "tb%d" % k)])
    if rank is None:
        for k in range(len(CHUNK)):
            TAB[k] = ("tb%d" % k, len(table_engines(k, [r for r in WAY[k] if role in WAY[k][r]][0])))
    else:
        table_on(0, NB[0])
    local, t_ld = False, None
    t_fs = None
    ri = vts(pidx[:, 2:3], pidx[:, 0:1], 15, None, ALU.bitwise_and, w=[g_pi])
    if rank is not None:
        hb = [q for q in (rank - 1, rank, rank + 1) if 0 <= q < NR]
        nc = 8 * len(hb)
        ca = 8 * hb[0]
        oi = vts(pidx[:, 1:2], pidx[:, 0:1], 4, None, ALU.arith_shift_right)
        vms(C("k1", 1, 0, 16), 0.0)
        c_rf = vcp(cst[:, 1:2], pidx[:, 2:3], w=[ri])
        c_of = vcp(cst[:, 0:1], pidx[:, 1:2], w=[oi])
        c_k1 = vms(C("k1", 1, 16, 128), 1024.0)
        c_th = vts(cst[:, 2:3], pidx[:, 1:2], 8192.0, None, ALU.mult)
        c_c0 = vts(cst[:, 4:5], pidx[:, 1:2], 0.0, 1024.0, ALU.is_equal, ALU.mult)
        vms(T.zo[:, 0, :], 0.0)
        c_nb = vts(cst[:, 5:6], cst[:, 4:5], -1024.0, None, ALU.add, w=[c_c0])
        s_ab = act(C("dlt"), C("cdv"), ACT.Abs, w=[g_cd, c_of], bias=cst[:, 0:1])
        c_zo = vms(T.zo[:, 1, :], 1.0)
        c_sx0 = vms(T.sx[:, 0:1], 0.0)
        vts(C("tri"), C("i16"), cst[:, 1:2], None, ALU.is_gt, w=[g_16, c_rf])
        rep = vts(C("rep"), C("i16"), cst[:, 1:2], None, ALU.is_equal)
        vts(C("e0"), C("dlt"), 0.0, 2.0, ALU.is_equal, ALU.mult, w=[s_ab])
        e_ = vts(C("e1"), C("dlt"), 1.0, -1.0, ALU.is_equal, ALU.mult)
        t_id = vcp(T.id16[:], C("rep", 16, 0, 16), w=[rep])
        c_2 = vtt(C("cd1"), C("e0"), C("e1"), ALU.add, w=[e_])
        t1 = vts(T.ei[:, 0, 0:nc], T.endw[:, ca:ca + nc], -4096.0 * rank, 0.0, ALU.add, ALU.max, w=[EN])
        c_3 = vms(C("cd1", 16, 0, 16), 1.0, w=[c_2])
        t2 = vts(T.ei[:, 1, 0:nc], T.ei[:, 0, 0:nc], 4096.0, None, ALU.min, w=[t1])
        c_cd = vtt(C("cd2"), C("cd1"), C("tri"), ALU.mult, w=[c_3])
        t3 = vts(T.ei[:, 2, 0:nc], T.ei[:, 1, 0:nc], 15, None, ALU.bitwise_and, w=[t2])
        c_zs = vms(T.zs[:], 0.0)
        t_rb = vcp(T.rbf[:, 0:nc], T.ei[:, 2, 0:nc], w=[t3])
        t_g = vts(T.gge[:], T.idxa[:], cst[:, 2:3], None, ALU.is_ge, w=[IA, c_th])
        mm(T.pd[:, 0:256], C("k1", 1), T.zo[0:1, 1, :], True, False, w=[c_k1, c_zo])
        mm(T.pd[:, 0:256], C("cd2"), T.gge[:], False, False, w=[c_cd, t_g])
        need("v", t_g, c_zo)
        t_s = do("v", V.tensor_tensor_scan, T.sx[:, 1:257], T.zo[:, 0, :], T.gge[:], 0.0, ALU.add, ALU.add)
        m_d = mm(T.pd[:, 0:256], C("cd1"), T.sx[:, 0:256], False, True, w=[t_s, c_sx0])
        for k in range(16):
            t_dg = act(T.rdg[:, 0:nc, k], T.rbf[:, 0:nc], ACT.Copy, w=[t_rb, t_id], scale=T.id16[:, k:k + 1])
        c_zs = vts(T.zs[:, 7:135:8], C("i16", 128, 0, 16), cst[:, 1:2], None, ALU.is_equal, w=[c_zs])
        t4 = vts(T.ei[:, 3, 0:nc], T.ei[:, 1, 0:nc], 4, None, ALU.arith_shift_right, w=[t2])
        whi, tb, mb = T.col[:, 0, :], T.col[:, 1, :], T.col[:, 2, :]
        p1 = vts(T.pv[:], T.idxe[:], 8191, None, ALU.bitwise_and, w=[IE])
        t_gd = vtt(T.gd[:], T.pd[:, 0:256], T.gge[:], ALU.mult, w=[m_d])
        p2 = vts(T.pay[:, 0, :], T.pv[:], -1.0, 8192.0, ALU.mult, ALU.add, w=[p1])
        t_cb = vcp(T.cbf[:, 0:nc], T.ei[:, 3, 0:nc], w=[t4])
        p3 = vcp(whi, T.pay[:, 0, :], w=[p2])
        p4 = vtt(T.col[:, 3, :], T.pay[:, 0, :], whi, ALU.subtract, w=[p3])
        p5 = do("v", V.reciprocal, T.pay[:, 2, :], whi)
        p6 = vtt(T.pay[:, 3, :], T.col[:, 3, :], T.pay[:, 2, :], ALU.mult, w=[p5, p4])
        for k in range(8):
            m_a = mm(T.pa[:, 0:32], T.zs[:, 7 - k:135 - k], T.gd[:, 32 * k:32 * k + 32], k == 0, k == 7, w=[t_gd, c_zs])
        m_r = mm(T.pr[:, 0:16 * nc], T.zo[0:16, 1, 0:128], T.rdg[:, 0:nc, :], True, True, w=[t_dg])
        m_c = mm(T.pn[:, 0:nc], C("rep", 16), T.cbf[:, 0:nc], True, True, w=[t_cb])
        s_pc = act(T.pc[:, 0:256], T.pd[:, 0:256], ACT.Identity, w=[m_d, t_gd, c_nb], bias=cst[:, 5:6])
        a1 = vts(T.ti[:], T.pa[:, 0:32], 1.0 / 128, -0.496, ALU.mult, ALU.add, w=[m_a])
        a2 = vts(tb, T.ti[:], -128.0, None, ALU.mult, w=[a1])
        a3 = vtt(mb, T.pa[:, 0:32], tb, ALU.add, w=[a2])
        tg = [(team[o][r], o) for o in range(NR) for r in range(len(SRC)) if SRC[r][0] <= rank < SRC[r][1] and team[o][r] != core]
        lag = {}

        def low_mm(j, stop):
            return mm(T.px[:, 0:64], T.oa[:, j, :], T.ob2[:, j, :], False, stop, w=[lag[j]])
        for k in range(32):
            vts(T.oa[:, k, :], C("iota_a"), T.col[:, 2, k:k + 1], None, ALU.is_equal, w=[a3, g_ia])
            o_b = vts(T.ob1[:, k, :], T.iota_b[:], T.col[:, 1, k:k + 1], T.col[:, 0, k:k + 1], ALU.is_equal, ALU.mult, w=[g_ib, p3])
            if k in VB:
                lag[k] = vts(T.ob2[:, k, :], T.iota_b[:], T.col[:, 1, k:k + 1], T.col[:, 3, k:k + 1], ALU.is_equal, ALU.mult, w=[p4])
            else:
                lag[k] = act(T.ob2[:, k, :], T.ob1[:, k, :], ACT.Copy, w=[o_b, p6], scale=T.pay[:, 3, k:k + 1])
            mm(T.px[:, 0:64], T.oa[:, k, :], T.ob1[:, k, :], k == 0, False, w=[o_b])
            if k >= LAG:
                low_mm(k - LAG, False)
            if k == KA:
                t_co = vcp(T.cof[:, 0:nc], T.pn[:, 0:nc], w=[m_c])
                t_p2 = vts(T.pc[:, 256:272], T.zo[:, 1, 0:16], cst[:, 4:5], None, ALU.mult)
                t_os = vts(T.osel[:], T.kc[:, KC.index("cdv"), 0:128:16], cst[:, 0:1], 0.0, ALU.add, ALU.is_le)
                t_ms = vms(T.msg[:], 0.0)
            if k == KA + 1:
                t_mk = vts(T.msk[:, 0:16 * nc], T.pr[:, 0:16 * nc], cst[:, 1:2], None, ALU.is_equal, w=[m_r])
            if k == KA + 3:
                t_mg = vtt(T.mg[:, 0:16 * nc], T.pc[:].indirect(T.cof[:, 0:nc]), T.msk[:, 0:16 * nc], ALU.mult,
                           w=[t_co, t_p2, s_pc, t_mk])
            if k == KA + 6:
                for j in range(len(hb)):
                    m_n = mm(T.pn[:, 128 + 8 * j:136 + 8 * j], T.mg[:, 128 * j:128 * j + 128], T.osel[:], True, True, w=[t_mg, t_os, t_co])
            if k == KA + 8:
                for j, q in enumerate(hb):
                    t_mc = vcp(T.msg[:, :, 8 + q - rank + 1], T.pn[:, 128 + 8 * j:136 + 8 * j], w=[m_n, t_ms])
                need("g", t_mc)
                send([(T.msg[:, o, 8:12], [(c, T.land[:, rank + 1, 8:12])], [e], "arc") for (c, o), e in zip(tg, es8)])
                table_on(NB[0], NB[1])
        for j in range(32 - LAG, 32):
            m_x = low_mm(j, j == 31)
        t_mx = vcp(T.msg[:, :, 0:8], T.px[:, 0:64], w=[m_x])
        need("g", t_mx)
        send([(T.msg[:, o, 0:8], [(c, T.land[:, rank + 1, 0:8])], [e], "arl") for (c, o), e in zip(tg, es8)])
        table_on(NB[1], len(CHUNK))
        local = s0 <= rank < s1
        if local:
            t_ld = vcp(T.land[:, rank + 1, :], T.msg[:, own, :], w=[t_mx, t_mc])
        t_fs = act(T.flg[:, 16:16 + 1024 * ns], T.oa[:, 0:8 * ns, :], ACT.Identity, w=[t_mx], bias=-LOW, scale=0.0)
    else:
        c_rf = vcp(cst[:, 1:2], pidx[:, 2:3], w=[ri])
        t_id = vts(T.id16[:], C("i16", 16, 0, 16), cst[0:16, 1:2], None, ALU.is_equal, w=[c_rf, g_16])
    sel_es = share(topo, team[own][MAKER], [team[own][0]] * 2)
    if rank is not None:
        t_sw = t_sp = ("sl", len(sel_es[0]) + len(sel_es[1]))
    else:
        for k in range(8):
            t_sw = vts(T.selw[:, k, :], C("dwr"), 16.0 * k, None, ALU.is_equal, w=[g_dw])
        for k in range(8):
            t_sp = vts(T.selp[:, k, :], C("dwr"), 16.0 * k - 1.0, None, ALU.is_equal)
        if role == MAKER:
            need("g", t_sw, t_sp)
            send([(x, [(team[own][0], x)], e, "sl") for x, e in zip((T.selw[:], T.selp[:]), sel_es)])
        table_on(0, len(CHUNK))
    z0 = vms(T.land[:, 0:s0 + 1, :], 0.0)
    z1 = vms(T.land[:, s1 + 1:10, :], 0.0)
    b_m = vts(T.qm[:, 3, 0:nq], T.qm[:, 3, 0:nq], 0.0, 15.0, ALU.max, ALU.add, w=[g_bm])
    b_w = vts(F("basew"), F("basew"), 0.0, 15.0, ALU.max, ALU.add, w=[g_bw])
    t_sx = vts(C("selx"), C("dwr"), 127.0, None, ALU.is_equal, w=[g_dw])
    t_lc = vms(T.tabx[:, 8192:8208], LOW)
    t_gc = vms(T.sc[:, 0:16], LOW)
    t_lt = vms(T.lowt[:, 0:128 * nq], LOW)
    t_fl = vms(T.flg[:, 0:16 + (1024 * ns if t_fs is None else 0)], -LOW)
    if role == ZMAKER:
        za = 0 if own > 0 else 1
        t_of = vms(T.onef[:], 1.0)
        z_m = vms(T.zsb[:, 0:16], 0.0)
        t_ef = vcp(T.ef[:, za:9], T.endw[:, 8 * own - 1 + za:8 * own + 8], w=[EN])
        for k in range(16):
            t_zd = act(T.zdg[:, za:9, k], T.ef[:, za:9], ACT.Copy, w=[t_ef, t_id], scale=T.id16[:, k:k + 1])
        m_z = mm(T.pr[:, 16 * za:144], T.onef[:], T.zdg[:, za:9, :], True, True, w=[t_zd, t_of])
        s_z = act(T.zsb[:, 16 * za:144], T.pr[:, 16 * za:144], ACT.Copy, w=[m_z, z_m])
        z_q = vtt(C("zt"), T.zsb[:, 16:144], T.zsb[:, 15:143], ALU.is_equal, w=[s_z, z_m])
        z_z = vts(C("zz"), C("zt"), -1.0, -LOW, ALU.add, ALU.mult, w=[z_q])
        need("g", z_z)
        send([(C("zz"), [(team[own][0], T.pland[:, 12, :])], share(topo, core, [team[own][0]])[0], "zl")])
    far = ns - (1 if local else 0)
    L = T.land
    qhi, qlw = T.qhl[:, 0, 0:nq], T.qhl[:, 1, 0:nq]
    q1 = vtt(T.qm[:, 0, 0:nq], L[:, qlo:qlo + nq, 10], L[:, qlo + 1:qlo + 1 + nq, 9], ALU.add, w=[z0, z1, t_ld, ("arc", far)])
    q2 = vtt(T.qm[:, 1, 0:nq], T.qm[:, 0, 0:nq], L[:, qlo + 2:qlo + 2 + nq, 8], ALU.add, w=[q1])
    q3 = vtt(T.qm[:, 2, 0:nq], T.qm[:, 1, 0:nq], T.qm[:, 3, 0:nq], ALU.add, w=[q2, b_m])
    q4 = vcp(qhi, T.qm[:, 2, 0:nq], w=[q3])
    q5 = vtt(qlw, T.qm[:, 2, 0:nq], qhi, ALU.subtract, w=[q4])
    for k in range(8):
        mm(T.pq[:, 0, k:2 * n8:8], T.selw[:, k, :], T.qhl[:, :, 0:nq], True, True, w=[q4, q5, t_sw])
        m_q = mm(T.pq[:, 1, k:2 * n8:8], T.selp[:, k, :], T.qhl[:, :, 0:nq], True, k > 0, w=[t_sp])
        if k == 0:
            mm(T.pq[:, 1, 8:n8:8], C("selx"), T.qhl[:, 0, 0:nq - 1], False, False, w=[t_sx])
            mm(T.pq[:, 1, n8 + 8:2 * n8:8], C("selx"), T.qhl[:, 1, 0:nq - 1], False, True)
    h1 = vcp(T.hsm[:, :, 0:n8], T.pq[:, :, 0:n8], w=[m_q])
    f0 = vtt(F("x2"), T.pq[:, 1, n8:2 * n8], T.hsm[:, 1, 0:n8], ALU.add, w=[h1])
    f9 = vtt(F("qq"), T.pq[:, 0, n8:2 * n8], T.hsm[:, 0, 0:n8], ALU.add)
    f1 = vtt(F("pm"), F("x2"), F("basew"), ALU.max, w=[f0, b_w])
    f2 = vtt(F("ee"), F("qq"), F("pm"), ALU.is_le, w=[f1, f9])
    f3 = vtt(F("xx"), F("ee"), F("trash"), ALU.mult, w=[f2, g_tr])
    f6 = vtt(T.lf[:, 0:n8], F("xx"), F("pm"), ALU.max, w=[f3])
    f7 = vcp(T.lfu[:, 0:n8], T.lf[:, 0:n8], w=[f6])
    f4 = vtt(F("x2"), F("ee"), F("qq"), ALU.mult)
    fw = 16 + 1024 * ns + 1136
    f5 = vtt(T.lf[:, 64:64 + n8], F("qq"), F("x2"), ALU.subtract, w=[f4])
    f8 = vcp(T.lfu[:, 64:64 + n8], T.lf[:, 64:64 + n8], w=[f5])

    def flags():
        return vcp(T.flg[:, 0:fw].indirect(T.lfu[:, 0:n8]), T.lowt[:, 0:128 * nq], w=[f7, t_fl, t_lt, t_fs])
    if rank is None:
        fl = flags()
    lhi, llo = T.lhl[:, 0, 0:8 * ns], T.lhl[:, 1, 0:8 * ns]
    w1 = vcp(lhi, L[:, s0 + 1:s1 + 1, 0:8], w=[("arl", far), t_ld])
    w2 = vtt(llo, L[:, s0 + 1:s1 + 1, 0:8], lhi, ALU.subtract, w=[w1])
    for k in range(8):
        mm(T.po[:, k:64 * ns:8], T.selw[:, k, :], lhi, True, False, w=[w1, t_sw])
        m_o = mm(T.po[:, k:64 * ns:8], T.selw[:, k, :], llo, False, True, w=[w2])
    w3 = vts(T.offs[:, 0:64 * ns], T.po[:, 0:64 * ns], -1.0, 8192.0, ALU.mult, ALU.add, w=[m_o])
    gth = [[] for k in range(ns)]

    def gather(a, b, vec):
        out, ind = T.gt[:, a:b], T.tabx[:].indirect(T.offs[:, a // 16:b // 16])
        w = TAB + [w3, t_lc]
        gth[a // 1024].append(vcp(out, ind, w=w) if vec else act(out, ind, ACT.Copy, w=w))
    cut = 1024 * ns - VECN[role]
    for k in range(ns):
        if 1024 * k < cut:
            gather(1024 * k, min(1024 * k + 1024, cut), False)
    if rank is not None:
        fl = flags()
    if cut < 1024 * ns:
        gather(cut, 1024 * ns, True)
    scn, done = [], {}

    def pick(q, vec):
        k = ready(role, q)
        win = T.sc[:, 0:1040 + 1024 * k].indirect(T.lfu[:, 64 + 8 * (q - qlo):72 + 8 * (q - qlo)])
        if vec:
            done[q] = vcp(T.part[:, q - qlo, :], win, w=[scn[k], f8])
        else:
            done[q] = act(T.part[:, q - qlo, :], win, ACT.Copy, w=[scn[k], f8])

    def pass_on(qs):
        if qs:
            red = [reducer(pair, q) for q in qs]
            idx = [4 * (q % 4 // 2) + inputs(pair, q).index((core, role)) for q in qs]
            need("g", *[done[q] for q in qs])
            send([(T.part[:, q - qlo, :], [(c, T.pland[:, i, :])], e, "ra%d" % i)
                  for q, c, e, i in zip(qs, red, share(topo, core, red), idx)])
    soon = [q for q in blk if early(role, q)]
    for k in range(ns):
        ini = LOW if k == 0 else T.sc[:, 15 + 1024 * k:16 + 1024 * k]
        need("v", fl, scn[k - 1] if k else t_gc, *gth[k])
        scn.append(do("v", V.tensor_tensor_scan, T.sc[:, 16 + 1024 * k:1040 + 1024 * k], T.flg[:, 15 + 1024 * k:1039 + 1024 * k],
                      T.gt[:, 1024 * k:1024 * k + 1024], ini, ALU.min, ALU.max))
        if soon and k == max(ready(role, q) for q in soon):
            for q in soon:
                pick(q, False)
            pass_on(outgoing(pair, core, role, True))
    out = outgoing(pair, core, role, False)
    for n, q in enumerate(out + [q for q in blk if q not in out and q not in done]):
        pick(q, n % 2 == 0)
    pass_on(out)
    t_red = {}
    for q in range(NR):
        if reducer(pair, q) != core:
            continue
        qi = q % 4 // 2
        ins = []
        for i, (c, r) in enumerate(inputs(pair, q)):
            if c == core:
                ins.append((T.part[:, q - qlo, :], done[q]))
            else:
                o = outgoing(pair, c, r, early(r, q))
                ins.append((T.pland[:, 4 * qi + i, :], ("ra%d" % (4 * qi + i), len(share(topo, c, [reducer(pair, x) for x in o])[0]))))
        acc, tok = ins[0]
        for i in range(1, len(ins)):
            res = T.red[:, qi, :] if i == len(ins) - 1 else (T.pp, T.pa)[qi][:, 0:128]
            tok = vtt(res, acc, ins[i][0], ALU.max, w=[tok, ins[i][1]])
            acc = res
        t_red[q] = tok
        if cores[q] != core:
            ci = chips.index(topo.chip(core))
            need("g", tok)
            send([(T.red[:, qi, :], [(cores[q], T.pland[:, 8 + ci, :])], share(topo, core, [cores[q]])[0], "fa%d" % ci)])
    if rank is not None:
        near, away = [(T.pland[:, 12, :], ("zl", len(share(topo, team[own][ZMAKER], [core])[0])))], []
        for ci, ch in enumerate(chips):
            c = reducer([t for t in team if topo.chip(t[0]) == ch], rank)
            if c == core:
                near.append((T.red[:, rank % 4 // 2, :], t_red[rank]))
            else:
                (near if ch == topo.chip(core) else away).append((T.pland[:, 8 + ci, :], ("fa%d" % ci, len(share(topo, c, [core])[0]))))
        ins = near + away
        acc, tok = ins[0]
        for i in range(1, len(ins)):
            res = T.ysb[:] if i == len(ins) - 1 else T.pd[:, 0:128]
            tok = vtt(res, acc, ins[i][0], ALU.max, w=[tok, ins[i][1]])
            acc = res
        need("y", tok)
        g.sync.dma_start(T.y[:], T.ysb[:]).then_inc(T.sem.yd, 16)
        need("y", ("yd", 16))
    need("g", *[(k, cnt[k]) for k in cnt])
